import numpy as np, ml_dtypes
CORES = [2,3,42,43,82,83,122,123]
N = 8
import mx_ref
BF = ml_dtypes.bfloat16
def pick(q, e):
    c = np.concatenate([q[0].reshape(128, -1, 4), np.zeros((128, 1, 4), np.uint8)], axis=1); s = np.concatenate([q[1], np.ones((16, 1), np.uint8)], axis=1)
    return (np.ascontiguousarray(c[:, e].reshape(128, -1)), np.ascontiguousarray(s[:, e]))
def join(*qs):
    return (np.concatenate([q[0] for q in qs], axis=1), np.concatenate([q[1] for q in qs], axis=1))
def put(q, e, v):
    c, s = q[0].reshape(128, -1, 4).copy(), q[1].copy(); c[:, e] = v[0].reshape(128, -1, 4); s[:, e] = v[1]
    return (c.reshape(128, -1), s)
def pk(c, s):
    return (np.ascontiguousarray(c), mx_ref.live(s))
def emit(q):
    return q[0], q[1]
def decode(q):
    o = []
    for b in range(4):
        e = np.zeros((128, 128, 4), np.float32); e[np.arange(128), np.arange(128), b] = 1
        o.append(mx_ref.matmul(mx_ref.quantize(e.reshape(128, 512).astype(BF)), q))
    return np.stack(o, axis=2).reshape(128, -1)
def f(rng, *shape):
    return mx_ref.flush((rng.standard_normal(shape, dtype=np.float32) * np.exp2(rng.integers(-2, 3, shape[:-1] + (1,)))).astype(BF))
def wide(rng, *shape, cols=0):
    v = rng.standard_normal(shape, dtype=np.float32) * np.exp2(rng.integers(-12, 13, shape)).astype(np.float32)
    if cols: v *= np.repeat(np.exp2(rng.integers(-cols, cols + 1, shape[:-2] + (1, shape[-1] // 4))) * (rng.random(shape[:-2] + (1, shape[-1] // 4)) > 0.0625), 4, axis=-1).astype(np.float32)
    return mx_ref.flush(v.astype(BF))
P, B, K, KO = 512, 64, 16, 16
def big(v):
    v = v.astype(np.float32)
    v[np.abs(v) < np.float32(2.0 ** -16)] = 0
    return v.astype(BF)
def toward(rng, u, size):
    sg = np.where(u[0, :, :4].astype(np.float32) < 0, -1.0, 1.0)
    s = np.asarray(size)[..., None, :, None]
    v = (1 + rng.random(s.shape[:-3] + (128, s.shape[-2], 4))) * sg[:, None, :] * s
    return v.reshape(v.shape[:-2] + (-1,)).astype(np.float32)
def near(rng, size):
    s = np.abs(np.asarray(size))[..., None, :, None]
    v = (rng.random(s.shape[:-3] + (128, s.shape[-2], 4)) - 0.5) * 0.25 * s
    return v.reshape(v.shape[:-2] + (-1,)).astype(np.float32)
def plain(rng):
    u = np.array(f(rng, 128, 512))
    u[:, 4:] = 0
    return {"gr": big(f(rng, N, 128, 4 * P)), "er": big(f(rng, N, 128, 4 * P).astype(np.float32) * np.float32(0.125)), "fo": big(f(rng, N, 128, 4 * B)), "u": np.stack([u] * N), "w": f(rng, N, 128, 512)}
def setup_inputs(rng):
    return plain(rng)
def setup_inputs_same(rng):
    d = plain(rng)
    size, own = np.full((B, N), 2.0 ** -5), np.full((N, B), 2.0 ** -4)
    for o in range(N):
        m = rng.permutation(B)
        size[m[:K], o] = np.exp2(rng.integers(0, 3, K))
        own[o, m[K:K + KO // 2]] = 2.0 ** 8
    size = size * rng.choice([-1.0, 1.0], size.shape)
    size = np.tile(size.reshape(P), (N, 1))
    own = own * rng.choice([-1.0, 1.0], own.shape)
    return {**d, "gr": big(toward(rng, d["u"], size)), "er": big(near(rng, size)), "fo": big(toward(rng, d["u"], own))}
def setup_inputs_apart(rng):
    d = plain(rng)
    size = np.full((N, B, N), 2.0 ** -5)
    for o in range(N):
        m, a = rng.permutation(B), rng.permutation(N)
        for s in range(N): size[s, m[(a[s] * K + np.arange(K)) % B], o] = np.exp2(rng.integers(0, 3, K))
    size = (size * rng.choice([-1.0, 1.0], size.shape)).reshape(N, P)
    e, fo = big(near(rng, size)), np.array(d["fo"])
    a = rng.permutation(N)
    e[a[0]] = 0
    fo[a[1]] = 0
    return {**d, "gr": big(toward(rng, d["u"], size)), "er": e, "fo": fo}
def setup_inputs_cancel(rng):
    d = plain(rng)
    size, own = np.full((B, N), 2.0 ** 5), np.full((N, B), 2.0 ** -13)
    gone = np.zeros(N, int)
    for o in range(N):
        m = rng.permutation(B)[:K]
        size[m, o] = np.exp2(rng.integers(11, 13, K))
        own[o, m] = np.exp2(rng.integers(-10, -8, K))
        own[o, m[:K // 2]] = 0
        gone[o] = m[K - 1]
    h = int(rng.integers(0, N))
    own[h] = 0
    size = np.tile(size.reshape(P), (N, 1)) * rng.choice([-1.0, 1.0], (N, P))
    g, e, fo = big(toward(rng, d["u"], size)), big(near(rng, size)), big(toward(rng, d["u"], own))
    a = rng.permutation(N)
    g[a[1::2]] = -g[a[::2]]
    e[a[1::2]] = -e[a[::2]]
    gv, ev, fv = g.reshape(N, 128, B, N, 4), e.reshape(N, 128, B, N, 4), fo.reshape(N, 128, B, 4)
    half = np.where(d["u"][0, :, :4].astype(np.float32) < 0, -1.0, 1.0) * 2.0 ** 11
    part = np.ones(N)
    part[a[1::2]] = -1
    part[a[:2]] = -1
    for o in range(N):
        if o == h: continue
        m, x = int(gone[o]), half * rng.choice([-1.0, 1.0])
        gv[:, :, m, o] = (part[:, None, None] * x).astype(BF)
        ev[:, :, m, o] = 0
        fv[o, :, m] = (2 * x).astype(BF)
    return {**d, "gr": g, "er": e, "fo": fo}
def setup_inputs_ties(rng):
    d = plain(rng)
    u = np.zeros((128, 512), BF)
    u[:, :4] = ((1 + rng.random((128, 4))) * 2.0 ** 29 * rng.choice([-1.0, 1.0], (128, 4))).astype(BF)
    d["u"] = np.stack([u] * N)
    size, own, tied = np.zeros((B, N)), np.ones((N, B)), np.zeros((N, B), bool)
    for o in range(N):
        t = int(rng.integers(2, min(K, KO)))
        m = rng.permutation(B)
        size[m[:t], o] = 2.0 ** 23
        size[int(m[:t].min()), o] = 7 * 2.0 ** 20
        own[o, m[:t]] = 2.0 ** 23
        tied[o, np.sort(m[t:])[K - t:]] = True
    size = np.tile(size.reshape(P), (N, 1))
    hot = np.repeat(size > 0, 4, axis=1)[:, None, :]
    sg = np.repeat(rng.choice([-1.0, 1.0], (N, P)), 4, axis=1)[:, None, :]
    g = np.where(hot, toward(rng, d["u"], size), np.tile(toward(rng, d["u"], np.ones((N, 1))), (1, 1, P)) * sg)
    e = np.where(hot, near(rng, size), np.tile(near(rng, np.ones((N, 1))), (1, 1, P)) * sg)
    so = np.repeat(rng.choice([-1.0, 1.0], (N, B)), 4, axis=1)[:, None, :]
    fo = np.where(np.repeat(tied, 4, axis=1)[:, None, :], np.tile(toward(rng, d["u"], np.full((N, 1), 2.0 ** 9)), (1, 1, B)) * so, toward(rng, d["u"], own))
    return {**d, "gr": big(g), "er": big(e), "fo": big(fo)}
def setup_inputs_spread(rng):
    g, e, fo = big(wide(rng, N, 128, 4 * P, cols=8)), big(wide(rng, N, 128, 4 * P, cols=8)), big(wide(rng, N, 128, 4 * B, cols=8))
    gv, ev, fv = g.reshape(N, 128, B, N, 4), e.reshape(N, 128, B, N, 4), fo.reshape(N, 128, B, 4)
    top = np.array([225.0, 241.0, 255.0])[np.arange(128) // 8 % 3][:, None]
    r = int(rng.integers(0, N))
    for o in range(N):
        z = np.sort(rng.permutation(B)[int(rng.integers(0, K)):])
        for v in (gv, ev):
            v[r][:, z, o] = 0
            v[:, :, int(z[0]), o] = 0
        fv[o, :, int(z[0])] = (top * np.exp2(rng.integers(-14, -10, (128, 4))) * rng.choice([-1.0, 1.0], (128, 4))).astype(BF)
    return {**plain(rng), "gr": g, "er": e, "fo": fo}
def check_inputs(d):
    b = []
    for k, lo, hi in (("gr", -16, 24), ("er", -16, 24), ("fo", -16, 24), ("u", -30, 30), ("w", -30, 30)):
        v = np.abs(d[k].astype(np.float32))
        if not (np.isfinite(v).all() and ((v == 0) | (v >= 2.0 ** lo) & (v <= 2.0 ** hi)).all()): b.append("a value of " + k)
    u = d["u"].astype(np.float32)
    if (u[:, :, 4:] != 0).any(): b.append("u has numbers behind its column 0")
    if (u != u[:1]).any(): b.append("u isn't the same on all ranks")
    return b
def best(z, k):
    return np.argsort(-np.abs(z), kind="stable")[:k]
def reference(gr, er, fo, u, w):
    oc, osc = np.zeros((N, 128, 4 * (P + B)), np.uint8), np.zeros((N, 16, P + B), np.uint8)
    nb, y = np.zeros((N, 1, N * KO), np.float32), np.zeros((N, 128, N * KO), np.float32)
    qu = [mx_ref.quantize(u[r]) for r in range(N)]
    sent, held, werr = [], [], []
    for s in range(N):
        v = (gr[s].astype(np.float32) + decode(mx_ref.quantize(er[s]))).astype(BF)
        q = mx_ref.quantize(v)
        z = mx_ref.matmul(qu[s], q)[0]
        e = [best(z[o::N], K) for o in range(N)]
        n = np.concatenate([N * e[o] + o for o in range(N)])
        dq = decode(q)
        left = mx_ref.quantize((v.astype(np.float32) - dq).astype(BF))
        werr.append(put(q, n, pick(left, n)))
        sent.append(e)
        held.append(dq.reshape(128, P, 4))
    win, numbers = [], []
    for o in range(N):
        qf = mx_ref.quantize(fo[o])
        a, named = decode(qf).reshape(128, B, 4).copy(), np.zeros(B, bool)
        for s in range(N):
            m = sent[s][o]
            a[:, m] = a[:, m] + held[s][:, N * m + o]
            named[m] = True
        a = a.reshape(128, 4 * B).astype(BF)
        m = np.flatnonzero(named)
        p = put(qf, m, pick(mx_ref.quantize(a), m))
        t = best(mx_ref.matmul(qu[o], p)[0], KO)
        left = mx_ref.quantize((a.astype(np.float32) - decode(p)).astype(BF))
        oc[o], osc[o] = emit(join(werr[o], put(p, t, pick(left, t))))
        win.append(pick(p, t))
        numbers.append(N * t + o)
    every = join(*win)
    for r in range(N):
        nb[r, 0] = np.concatenate(numbers)
        y[r] = mx_ref.matmul(mx_ref.quantize(w[r]), every)
    return {"oc": oc, "osc": osc, "nb": nb, "y": y}

@@ -1,0 +1,597 @@
+import numpy as np
+from concourse.bass import DstId, RemoteDMATransfer
+from concourse.mybir import dt, AluOpType, AxisListType, ActivationFunctionType
+
+CODE = "float8_e4m3fn_x4"
+BFT = "bfloat16"
+F32 = "float32"
+Q0 = 160
+OH1 = Q0 + 512
+LEFT = 704
+BLK = 32
+MSG = 18
+HALF = 112
+WIN = 17
+TINY = 2.0 ** -120
+
+SCRATCH = {
+    "ert": ("sbuf", [128, 2048], BFT), "grt": ("sbuf", [128, 2048], BFT), "fz": ("sbuf", [128, 512], BFT),
+    "uc": ("sbuf", [128, 4], BFT), "ut": ("sbuf", [128, 512], BFT), "wt": ("sbuf", [128, 512], BFT),
+    "ones": ("sbuf", [128, 128], BFT), "idn": ("sbuf", [128, 128], BFT), "eb": ("sbuf", [128, 2048], BFT),
+    "ebq": ("sbuf", [128, 512], CODE), "ebs": ("sbuf", [128, 512], "uint8"),
+    "zq": ("sbuf", [128, 128], CODE), "zs": ("sbuf", [128, 128], "uint8"),
+    "ci": ("sbuf", [128, 32], "int32"), "cf": ("sbuf", [128, 112], F32), "z8": ("sbuf", [128, 8], F32),
+    "c64": ("sbuf", [128, 64], F32), "b32": ("sbuf", [128, 32], F32), "lf": ("sbuf", [128, 64], F32),
+    "i16": ("sbuf", [128, 128], BFT), "iadj": ("sbuf", [128, 128], BFT), "sm": ("sbuf", [128, 512], BFT),
+    "ct1": ("sbuf", [128, 544], BFT), "c1q": ("sbuf", [128, 136], CODE), "c1s": ("sbuf", [128, 136], "uint8"),
+    "ct": ("sbuf", [128, 1024], BFT), "ctq": ("sbuf", [128, 256], CODE), "cts": ("sbuf", [128, 256], "uint8"),
+    "cn": ("sbuf", [128, 2048], BFT), "cnq": ("sbuf", [128, 512], CODE), "cns": ("sbuf", [128, 512], "uint8"),
+    "lvo": ("sbuf", [128, 8], "uint16"), "zo": ("sbuf", [128, 4], "uint16"),
+    "erq": ("sbuf", [128, 512], CODE), "ers": ("sbuf", [128, 512], "uint8"),
+    "uq": ("sbuf", [128, 128], CODE), "us": ("sbuf", [128, 128], "uint8"),
+    "wq": ("sbuf", [128, 128], CODE), "ws": ("sbuf", [128, 128], "uint8"),
+    "v": ("sbuf", [128, 2048], BFT), "qb": ("sbuf", [128, 1376], CODE), "qs": ("sbuf", [128, 1376], "uint8"),
+    "sce": ("sbuf", [128, 272], F32), "tt": ("sbuf", [128, 256], F32),
+    "cmp": ("sbuf", [128, 256], F32), "rk": ("sbuf", [128, 4], F32),
+    "oht0": ("sbuf", [128, 528], BFT), "oht1": ("sbuf", [128, 528], BFT),
+    "ol0": ("sbuf", [128, 8], "uint16"), "ol1": ("sbuf", [128, 8], "uint16"),
+    "snd": ("sbuf", [128, 2 * HALF], CODE), "sns": ("sbuf", [128, 2 * HALF], "uint8"),
+    "lft": ("sbuf", [128, 2048], BFT), "ff": ("sbuf", [128, 4], F32), "fmw": ("sbuf", [128, 512], BFT),
+    "fwq": ("sbuf", [128, 128], CODE), "fws": ("sbuf", [128, 128], "uint8"), "fo32": ("sbuf", [128, 32], F32),
+    "fol": ("sbuf", [128, 32], "uint16"), "fin": ("sbuf", [128, 512], CODE), "fis": ("sbuf", [128, 512], "uint8"),
+    "fs": ("sbuf", [128, 2048], BFT), "fsq": ("sbuf", [128, 512], CODE), "fss": ("sbuf", [128, 512], "uint8"),
+    "l1": ("sbuf", [128, 256], CODE), "l1s": ("sbuf", [128, 256], "uint8"),
+    "lvq": ("sbuf", [128, 128], CODE), "lvs": ("sbuf", [128, 128], "uint8"),
+    "dol": ("sbuf", [128, 32], "uint16"), "dq": ("sbuf", [128, 512], CODE), "dqs": ("sbuf", [128, 512], "uint8"),
+    "so": ("sbuf", [128, 2048], BFT), "at": ("sbuf", [128, 512], BFT),
+    "pb": ("sbuf", [128, 256], CODE), "pbs": ("sbuf", [128, 256], "uint8"),
+    "njk": ("sbuf", [128, 16], F32), "nsum": ("sbuf", [128, 4], F32), "nsg": ("sbuf", [128, 4], F32),
+    "nof": ("sbuf", [128, 4], F32), "pol": ("sbuf", [128, 4], "uint16"),
+    "pp": ("sbuf", [128, 256], CODE), "pps": ("sbuf", [128, 256], "uint8"),
+    "sce2": ("sbuf", [128, 65], F32), "tt2": ("sbuf", [128, 64], F32),
+    "cmp2": ("sbuf", [128, 64], F32), "rk2": ("sbuf", [128, 2], F32), "oh2": ("sbuf", [128, 512], BFT),
+    "ohq": ("sbuf", [128, 128], CODE), "ohs": ("sbuf", [128, 128], "uint8"),
+    "wol": ("sbuf", [128, 2], "uint16"), "nt": ("sbuf", [128, 512], BFT),
+    "w2": ("sbuf", [128, 144], CODE), "w2s": ("sbuf", [128, 144], "uint8"),
+    "l2": ("sbuf", [128, 136], CODE), "l2s": ("sbuf", [128, 136], "uint8"),
+    "lpt": ("sbuf", [128, 512], BFT), "fm": ("sbuf", [128, 512], BFT),
+    "fmq": ("sbuf", [128, 128], CODE), "fms": ("sbuf", [128, 128], "uint8"), "go4": ("sbuf", [128, 4], F32),
+    "gol": ("sbuf", [128, 4], "uint16"), "gin": ("sbuf", [128, 64], CODE), "gis": ("sbuf", [128, 64], "uint8"),
+    "oci": ("sbuf", [128, 2], "int32"), "nbs": ("sbuf", [128, 16], F32), "yo": ("sbuf", [128, 128], F32),
+}
+for _k in range(8):
+    SCRATCH["P%d" % _k] = ("psum", [128, 512], F32)
+NDMA = 40
+SEMAPHORES = ["v", "s", "t", "gp", "arr1", "arr2", "lcl"] + ["d%d" % i for i in range(NDMA)]
+
+
+def at(name, a, b, st=1, p0=0, p1=128):
+    return (name, a, b, st, p0, p1)
+
+
+def hit(x, y):
+    if x[0] != y[0] or x[4] >= y[5] or y[4] >= x[5] or x[1] >= y[2] or y[1] >= x[2]:
+        return False
+    return not (x[3] == y[3] and (x[1] - y[1]) % x[3] != 0)
+
+
+def make_flow(g, T):
+    queues = {"v": g.vector, "s": g.scalar, "t": g.tensor, "gp": g, "y": g.sync}
+    count, know, hist, ndma = {}, {q: {} for q in queues}, {}, [0]
+
+    def ap(r):
+        return T[r[0]][r[4]:r[5], r[1]:r[2]] if r[3] == 1 else T[r[0]][r[4]:r[5], r[1]:r[2]:r[3]]
+
+    def need(q, reads, writes, chain=False):
+        toks = []
+        for mode, rs in (("r", reads), ("w", writes)):
+            for r in rs:
+                for (q2, m2, r2, tok, ch) in hist.get(r[0], []):
+                    bank = r[0][0] == "P"
+                    if bank:
+                        if q2 == q and m2 == "r" and mode == "r":
+                            continue
+                        if q2 == q and chain:
+                            continue
+                    elif (mode == "r" and m2 == "r") or not hit(r, r2):
+                        continue
+                    toks.append(tok)
+        for sem, n, kn in sorted(toks, key=lambda x: -x[1]):
+            if know[q].get(sem, 0) < n:
+                queues[q].wait_ge(T.sem[sem], n)
+                know[q][sem] = n
+                for s2, n2 in kn.items():
+                    know[q][s2] = max(know[q].get(s2, 0), n2)
+
+    def note(q, reads, writes, tok, chain=False):
+        for mode, rs in (("r", reads), ("w", writes)):
+            for r in rs:
+                h = hist.setdefault(r[0], [])
+                if mode == "w" and not chain:
+                    h[:] = [e for e in h if not (r[0][0] == "P" or (e[2][3] == 1 and r[3] == 1 and r[1] <= e[2][1]
+                            and e[2][2] <= r[2] and r[4] <= e[2][4] and e[2][5] <= r[5]))]
+                h.append((q, mode, r, tok, chain))
+
+    def op(q, call, reads, writes, chain=False):
+        need(q, reads, writes, chain)
+        if q == "gp" and know[q].get(q, 0) < count.get(q, 0):
+            g.wait_ge(T.sem[q], count[q])
+            know[q][q] = count[q]
+        ins = call()
+        count[q] = count.get(q, 0) + 1
+        ins.then_inc(T.sem[q], 1)
+        note(q, reads, writes, (q, count[q], dict(know[q])), chain)
+
+    def dma(q, out, in_, reads, writes):
+        need(q, reads, writes)
+        sem = "d%d" % ndma[0]
+        ndma[0] += 1
+        queues[q].dma_start(out, in_).then_inc(T.sem[sem], 16)
+        count[sem] = 16
+        note(q, reads, writes, (sem, 16, dict(know[q])))
+
+    def lands(sem, n, writes):
+        count[sem] = n
+        note("far", [], writes, (sem, n, {}), True)
+
+    def finish(extra):
+        for sem, n in list(count.items()) + extra:
+            if know["y"].get(sem, 0) < n:
+                g.sync.wait_ge(T.sem[sem], n)
+
+    return ap, need, op, dma, lands, finish
+
+
+def ways(T, topo, src):
+    far = [d for d in T.cores if topo.chip(d) != topo.chip(src)]
+    near = [d for d in T.cores if topo.chip(d) == topo.chip(src) and d != src]
+    e = topo.engines(src, far[0])
+    return far, near, e, [x for x in topo.engines(src, near[0]) if x not in e][:4]
+
+
+def plan1(T, topo, src):
+    r = T.rank_of(src)
+    far, near, e, ne = ways(T, topo, src)
+    res = {}
+    for half in (1 - r // 4, r // 4):
+        ds = [d for d in far if T.rank_of(d) // 4 == half]
+        n = len(e) // len(ds)
+        for i, d in enumerate(ds):
+            res[d] = (half, e[n * i:n * i + n])
+    for d in near:
+        res[d] = (T.rank_of(d) // 4, ne)
+    return res
+
+
+def bits(es):
+    return sum(1 << x for x in es)
+
+
+def rank_program(g, core, T, topo):
+    me = T.rank_of(core)
+    if me is None:
+        return
+    N = len(T.cores)
+    ap, need, op, dma, lands, finish = make_flow(g, T)
+    A = AluOpType
+    ACT = ActivationFunctionType
+    odd, ot = me % 2, me // 2 % 2
+    h0, h1 = 64 * odd, 64 * odd + 64
+
+    def ts(out, in0, s1, op0, s2=None, op1=None):
+        reads = [in0] + [x for x in (s1, s2) if x is not None and not isinstance(x, (int, float))]
+        a1 = s1 if isinstance(s1, (int, float)) else ap(s1)
+        a2 = s2 if s2 is None or isinstance(s2, (int, float)) else ap(s2)
+        if op1 is None:
+            op("v", lambda: g.vector.tensor_scalar(ap(out), ap(in0), a1, None, op0), reads, [out])
+        else:
+            op("v", lambda: g.vector.tensor_scalar(ap(out), ap(in0), a1, a2, op0, op1), reads, [out])
+
+    def tt(out, in0, in1, o):
+        op("v", lambda: g.vector.tensor_tensor(ap(out), ap(in0), ap(in1), o), [in0, in1], [out])
+
+    def cp(out, in_):
+        op("v", lambda: g.vector.tensor_copy(ap(out), ap(in_)), [in_], [out])
+
+    def fill(out, c):
+        op("v", lambda: g.vector.memset(ap(out), c), [], [out])
+
+    def total(out, in_):
+        op("v", lambda: g.vector.tensor_reduce(ap(out), ap(in_), AxisListType.X, A.add), [in_], [out])
+
+    def act(out, in_, f, bias=0.0, scale=1.0, acc=None):
+        reads = [in_] + [x for x in (bias, scale) if not isinstance(x, float)]
+        kw = {}
+        if not (isinstance(bias, float) and bias == 0.0):
+            kw["bias"] = bias if isinstance(bias, float) else ap(bias)
+        if not (isinstance(scale, float) and scale == 1.0):
+            kw["scale"] = scale if isinstance(scale, float) else ap(scale)
+        if acc is not None:
+            kw["accum_out"] = ap(acc)
+        op("s", lambda: g.scalar.activation(ap(out), ap(in_), f, **kw), reads, [out] + ([acc] if acc else []))
+
+    def quant(q, s, a, b, src, c):
+        n = b - a
+        i = at(src, c, c + 4 * n)
+        op("v", lambda: g.vector.quantize_mx(ap(at(q, a, b)), ap(at(s, a, b)), ap(i)), [i], [at(q, a, b), at(s, a, b)])
+
+    def mm(bank, n, w, a, x, b, start=True, stop=True):
+        o, l, r = at(bank, 0, n), (at(w[0], a, a + 128), at(w[1], a, a + 128)), (at(x[0], b, b + n), at(x[1], b, b + n))
+        op("t", lambda: g.tensor.matmul_mx(ap(o), ap(l[0]), ap(l[1]), ap(r[0]), ap(r[1]), start, stop),
+           list(l) + list(r), [o], chain=not start)
+
+    def pick(q2, s2, a2, q, s, a, b, off, e, f):
+        n = 16 * (f - e)
+        lst, wq, wsc, oq, osc = at(off, e, f), at(q, a, b), at(s, a, b), at(q2, a2, a2 + n), at(s2, a2, a2 + n)
+        op("v", lambda: g.vector.tensor_copy(ap(oq).bitcast(dt.uint32), ap(wq).bitcast(dt.uint32).indirect(ap(lst))),
+           [wq, lst], [oq])
+        op("s", lambda: g.scalar.activation(ap(osc), ap(wsc).indirect(ap(lst)), ACT.Copy), [wsc, lst], [osc])
+
+    def zeros(*regions):
+        for name, a, b in regions:
+            act(at(name, a, b), at("eb", 0, b - a), ACT.Copy, scale=0.0)
+
+    def codes(r):
+        return ap(r).bitcast(dt.uint8)
+
+    def load(q, t, a, b, x):
+        dma(q, ap(at(t, a, b)), x, [], [at(t, a, b)])
+
+    def iota(out, pattern, base, ch):
+        if SCRATCH[out[0]][2] in (F32, BFT):
+            op("gp", lambda: g.iota(ap(out), pattern, base, ch, allow_small_or_imprecise_dtypes=True), [], [out])
+        else:
+            op("gp", lambda: g.iota(ap(out), pattern, base, ch), [], [out])
+
+    def ibit(a, o0, s0, o1=None, s1=None):
+        ts(at("ci", a, a + 4), at("ci", 0, 4), s0, o0, s1, o1)
+
+    def col(a, p0=0, p1=128):
+        return at("cf", a, a + 1, 1, p0, p1)
+    P_, M_, LO, I_, E_, H_, MH, I3 = 0, 4, 8, 12, 16, 20, 24, 28
+    K16, C2, MD, MK, TG, E8, MKM, EV, CON, LVC, M16, MKB, MIDS, OC, OB, HB, MID = \
+        32, 40, 44, 48, 52, 56, 60, 64, 65, 66, 67, 68, 72, 77, 78, 80, 82
+    EB, U, Q, C1, CT, PP, L2 = ("ebq", "ebs"), ("uq", "us"), ("qb", "qs"), ("c1q", "c1s"), ("ctq", "cts"), \
+        ("pp", "pps"), ("l2", "l2s")
+    far, near, fe, ne = ways(T, topo, core)
+    nloc = [0]
+
+    load("y", "ert", 0, 1024, T.er[:, 0:1024])
+    load("s", "ert", 1024, 2048, T.er[:, 1024:2048])
+    load("y", "uc", 0, 4, T.u[:, 0:4])
+    load("y", "grt", 0, 1024, T.gr[:, 0:1024])
+    load("s", "grt", 1024, 2048, T.gr[:, 1024:2048])
+    load("y", "fz", 0, 256, T.fo[:])
+    load("y", "wt", 0, 512, T.w[:])
+
+    fill(at("ones", 0, 128), 1.0)
+    fill(at("oht0", 0, 528), 0.0)
+    op("gp", lambda: g.affine_select(ap(at("idn", 0, 128)), ap(at("ones", 0, 128)), [[-1, 128]], A.is_equal, 0.0, 0, 1),
+       [at("ones", 0, 128)], [at("idn", 0, 128)])
+    iota(at("ci", 0, 4), [[0, 4]], 0, 1)
+    iota(at("c64", 0, 64), [[1, 64]], 0, 0)
+    quant("zq", "zs", 0, 128, "oht0", 0)
+    fill(at("eb", 0, 2048), 0.0)
+    for b in range(4):
+        act(at("eb", 512 * b + b, 512 * b + 512, 4), at("idn", 0, 128), ACT.Copy)
+    ibit(M_, A.bitwise_and, 63)
+    ibit(LO, A.bitwise_and, 7)
+    ibit(I_, A.bitwise_and, 15)
+    ibit(E_, A.bitwise_and, 1)
+    ibit(H_, A.arith_shift_right, 6)
+    ibit(MH, A.bitwise_and, 63, A.arith_shift_right, 1)
+    ibit(I3, A.bitwise_and, 15, A.arith_shift_right, 3)
+    quant("ebq", "ebs", 0, 512, "eb", 0)
+    cp(at("cf", 0, 32), at("ci", 0, 32))
+
+    def zslot(o):
+        return BLK * me + (0 if o % 2 else MSG)
+    for buf, land, f in (("zq", "l1", codes), ("zs", "l1s", ap)):
+        src = at(buf, 0, 2)
+        trs = []
+        for ds, es in ((far, fe), (near, ne)):
+            ids, dsts = [], []
+            for d in ds:
+                rid, pid, _ = topo.addr(d)
+                ids.append(DstId(rid=rid, pnc=pid))
+                z = zslot(T.rank_of(d))
+                dsts.append(f(at(land, z, z + 2)))
+            trs.append(RemoteDMATransfer(dst_ids=ids, dma_engine_mask=bits(es), remote_sem=T.sem.arr1,
+                                         srcs=[f(src)], dsts=dsts))
+        need("gp", [src], [])
+        g.remote_dma_fused(trs, local_sem=T.sem.lcl)
+        nloc[0] += len(fe) + len(ne)
+        z = at(land, zslot(me), zslot(me) + 2)
+        dma("y", f(z), f(src), [src], [z])
+    iota(at("iadj", 0, 128, 1, 0, 64), [[0, 8], [1, 16]], 0, 0)
+    iota(at("iadj", 0, 128, 1, 64, 128), [[0, 8], [-1, 16]], 15, 0)
+    iota(at("cf", 40, 44), [[2, 4]], 0, 0)
+    iota(at("cf", 32, 36), [[16, 4]], 0, 0)
+    iota(at("i16", 0, 128), [[0, 8], [1, 16]], 0, 0)
+    iota(at("b32", 0, 32), [[2, 32]], 0, 0)
+    iota(at("ct", 0, 1024), [[0, 1024]], 0, 0)
+    zeros(("ct1", 0, 544), ("oht1", 0, 528))
+    fill(at("z8", 0, 8), 0.0)
+    ts(at("lf", 0, 64), at("c64", 0, 64), col(M_), A.is_lt, -(2.0 ** -24), A.mult)
+    ts(col(EV), col(E_), -1.0, A.mult, 1.0, A.add)
+    tt(col(HB), col(P_), col(I_), A.subtract)
+    ts(at("lf", 0, 64), at("lf", 0, 64), 1.0, A.add)
+    for j, (i, k) in enumerate(((0, -2.0), (1, -1.0), (14, -2.0), (15, -1.0))):
+        ts(col(MIDS + j), col(I_), float(i), A.is_equal, k, A.mult)
+    ts(col(HB + 1), col(HB), 128.0, A.add)
+    for s, b in ((I_, 0), (HB, 32)):
+        act(at("ct1", b + 4, b + 18, 13, 0, 64), at("cf", s, s + 2, 1, 0, 64), ACT.Copy)
+        act(at("ct1", b + 8, b + 22, 13, 64, 128), at("cf", s, s + 2, 1, 64, 128), ACT.Copy)
+    zeros(("fs", 0, 2048), ("cn", 0, 1024))
+
+    quant("erq", "ers", 0, 256, "ert", 0)
+    quant("erq", "ers", 256, 512, "ert", 1024)
+    for b in range(4):
+        mm("P%d" % b, 512, EB, 128 * b, ("erq", "ers"), 0)
+    for t in range(4):
+        ts(at("ut", t, 512, 4), at("ones", 0, 128), at("uc", t, t + 1), A.mult)
+    total(col(MID), at("cf", MIDS, MIDS + 4))
+    quant("uq", "us", 0, 128, "ut", 0)
+    quant("c1q", "c1s", 0, 136, "ct1", 0)
+    ts(at("ol0", 0, 7, 3), at("z8", 0, 3), col(MID), A.add, 130.0, A.add)
+    ts(at("ol1", 0, 7, 3), at("z8", 0, 3), col(MID), A.add, float(OH1 - Q0 - 256 + 130), A.add)
+
+    def vadd(b, *owners):
+        for o in owners:
+            tt(at("v", 256 * o + b, 256 * o + 256, 4), at("P%d" % b, o, 512, N), at("grt", 4 * o + b, 2048, 4 * N), A.add)
+
+    def scored(c, p1, p2):
+        a, k = Q0 + 128 * c, 68 * c
+        quant("qb", "qs", a, a + 128, "v", 512 * c)
+        mm(p1, 128, Q, a, U, 0)
+        mm(p2, 128, U, 0, Q, a)
+        act(at("sce", k + 64, k + 65), at(p1, 0, 1), ACT.Abs, bias=TINY)
+        act(at("sce", k, k + 64, 1, 0, 64), at(p2, 0, 64, 1, 0, 64), ACT.Abs, bias=TINY)
+        act(at("sce", k, k + 64, 1, 64, 128), at(p2, 64, 128, 1, 64, 128), ACT.Abs, bias=TINY)
+        act(at("tt", 64 * c, 64 * c + 64), at("lf", 0, 64), ACT.Copy, scale=at("sce", k + 64, k + 65))
+
+    def beats(c):
+        tt(at("cmp", 64 * c, 64 * c + 64), at("sce", 68 * c, 68 * c + 64), at("tt", 64 * c, 64 * c + 64), A.is_gt)
+
+    def ranks(c):
+        total(at("rk", c, c + 1), at("cmp", 64 * c, 64 * c + 64))
+
+    def onehot(c):
+        ts(at("oht%d" % (c // 2), c % 2, 512, 4), at("iadj", 0, 128), at("rk", c, c + 1), A.is_equal)
+
+    def listed(h, bank):
+        oh, r = "oht%d" % h, at("rk", 2 * h, 2 * h + 2)
+        ts(at(oh, 512, 514), r, 16.0, A.min, col(EV), A.mult)
+        ts(at(oh, 516, 518), r, 16.0, A.min, col(E_), A.mult)
+        a = OH1 * h
+        quant("qb", "qs", a, a + 132, oh, 0)
+        mm(bank, 128, Q, a, C1, 0, True, False)
+        mm(bank, 128, Q, a, C1, 8, False, True)
+
+    def offsets(h, bank):
+        for j in (1, 4):
+            ts(at("ol%d" % h, j, j + 2), at(bank, j, j + 2), 0.0 if h else float(Q0), A.add)
+
+    def picked(h):
+        a, b = (Q0 + 256, OH1 + 132) if h else (0, Q0 + 256)
+        pick("snd", "sns", HALF * h, "qb", "qs", a, b, "ol%d" % h, 0, 7)
+
+    def slot(o):
+        return HALF * (o // 4) + 48 * (o // 2 % 2) + (32 if o % 2 else 14)
+
+    def lslot(o):
+        return BLK * me + (2 if o % 2 else 0)
+    plan = plan1(T, topo, core)
+
+    def sent(half):
+        for buf, land, f in (("snd", "l1", codes), ("sns", "l1s", ap)):
+            trs, rs = [], []
+            for d in plan:
+                if plan[d][0] == half:
+                    o = T.rank_of(d)
+                    r, l = at(buf, slot(o), slot(o) + MSG), at(land, lslot(o), lslot(o) + MSG)
+                    rid, pid, _ = topo.addr(d)
+                    trs.append(RemoteDMATransfer(dst_ids=[DstId(rid=rid, pnc=pid)], dma_engine_mask=bits(plan[d][1]),
+                                                 remote_sem=T.sem.arr1, src=f(r), dst=f(l)))
+                    rs.append(r)
+                    nloc[0] += len(plan[d][1])
+            need("gp", rs, [])
+            g.remote_dma_fused(trs, local_sem=T.sem.lcl)
+
+    first, second = 1 - me // 4, me // 4
+    cA, cB, cC, cD = 2 * first, 2 * first + 1, 2 * second, 2 * second + 1
+    of, os_ = range(4 * first, 4 * first + 4), range(4 * second, 4 * second + 4)
+    for b in range(3):
+        vadd(b, *of)
+    vadd(0, *os_)
+    vadd(3, 2 * cA, 2 * cA + 1)
+    scored(cA, "P4", "P5")
+    vadd(3, 2 * cB, 2 * cB + 1)
+    scored(cB, "P6", "P7")
+    vadd(1, *os_)
+    vadd(2, *os_)
+    beats(cA)
+    vadd(3, 2 * cC)
+    beats(cB)
+    ranks(cA)
+    vadd(3, 2 * cC + 1)
+    ranks(cB)
+    onehot(cA)
+    scored(cC, "P4", "P5")
+    onehot(cB)
+    listed(first, "P0")
+    vadd(3, 2 * cD, 2 * cD + 1)
+    scored(cD, "P6", "P7")
+    beats(cC)
+    offsets(first, "P0")
+    ranks(cC)
+    picked(first)
+    sent(first)
+    onehot(cC)
+    beats(cD)
+    ranks(cD)
+    onehot(cD)
+    listed(second, "P1")
+    ts(at("cf", MKM, MKM + 4), at("cf", K16, K16 + 4), -1.0, A.mult, col(M_), A.add)
+    tt(at("cf", MD, MD + 4), at("cf", M_, M_ + 4), at("cf", LO, LO + 4), A.subtract)
+    tt(col(M16), col(M_), col(I_), A.subtract)
+    ts(col(CON), col(LO), float(BLK), A.mult, 17.0 if odd else 2.0, A.add)
+    ts(col(LVC), col(LO), float(BLK), A.mult, col(I3), A.add)
+    offsets(second, "P1")
+    ts(col(E8), col(E_), 8.0, A.mult)
+    ts(at("lvo", 0, 8), at("z8", 0, 8), col(LVC), A.add, 18.0 if odd else 0.0, A.add)
+    picked(second)
+    ts(at("cf", TG, TG + 4), at("cf", C2, C2 + 4), col(H_), A.add, col(E8), A.add)
+    sent(second)
+    mine, mine_s = at("snd", slot(me), slot(me) + MSG), at("sns", slot(me), slot(me) + MSG)
+    home, home_s = at("l1", lslot(me), lslot(me) + MSG), at("l1s", lslot(me), lslot(me) + MSG)
+    dma("y", codes(home), codes(mine), [mine], [home])
+    dma("y", ap(home_s), ap(mine_s), [mine_s], [home_s])
+    n1 = 0
+    for s in T.cores:
+        if s != core:
+            f2, n2_, e2, ne2 = ways(T, topo, s)
+            n1 += 2 * len(plan1(T, topo, s)[core][1]) + 2 * len(e2 if core in f2 else ne2)
+
+    zeros(("cn", 1024, 2048), ("fz", 256, 512))
+    for b in range(4):
+        act(at("fs", b, 2048, 32), at("fz", b, 256, 4), ACT.Copy)
+    act(at("sm", 0, 512), at("eb", 0, 512), ACT.Identity, bias=1.0, scale=0.0)
+    act(at("sm", 0, 512, 8), at("eb", 0, 64), ACT.Copy, scale=0.0)
+    for name, a, b in (("at", 256, 512), ("oh2", 0, 512), ("nt", 0, 512), ("fm", 0, 512)):
+        iota(at(name, a, b), [[0, b - a]], 0, 0)
+    ts(at("ct", 144 + ot, 144 + 128, 4, h0, h1), at("c64", 0, 32, 1, h0, h1), col(MH, h0, h1), A.is_equal,
+       -1.0 if odd else 1.0, A.mult)
+    cp(at("ct", 276, 277, 1, 0, 64), at("cf", LO, LO + 1, 1, 0, 64))
+    cp(at("ct", 272, 273, 1, 0, 64), at("cf", MD, MD + 1, 1, 0, 64))
+    for t in range(4):
+        ts(at("ct", 304 + t, 304 + 128, 4), at("c64", 0, 32), col(MH), A.is_equal, float(LEFT), A.mult)
+    ts(at("ct", 432, 448, 4, 0, 64), at("cf", K16, K16 + 4, 1, 0, 64), col(M16, 0, 64), A.is_equal, 128.0, A.mult)
+    for t in range(2):
+        ts(at("ct", 448 + t, 448 + 64, 4), at("c64", 0, 16), col(P_), A.is_equal)
+    quant("ctq", "cts", 0, 256, "ct", 0)
+    ts(at("cf", MK, MK + 4), at("cf", K16, K16 + 4), col(I_), A.add)
+    ts(at("cf", MKB, MKB + 4), at("cf", K16, K16 + 4), col(I_), A.add, 64.0, A.add)
+    ts(at("zo", 0, 4), at("z8", 0, 4), 64.0, A.add)
+    quant("pb", "pbs", 0, 128, "fz", 0)
+    quant("fsq", "fss", 0, 512, "fs", 0)
+    for b in range(4):
+        mm("P%d" % b, 512, EB, 128 * b, ("fsq", "fss"), 0, True, False)
+    for k in range(4):
+        ts(at("cn", 512 * k + ot, 512 * k + 512, 4, h0, h1), at("i16", 0, 128, 1, h0, h1), col(MKM + k, h0, h1), A.is_equal)
+    pick("pp", "pps", 64, "pb", "pbs", 0, 128, "zo", 0, 4)
+    quant("cnq", "cns", 0, 512, "cn", 0)
+
+    lands("arr1", n1, [at("l1", 0, 256), at("l1s", 0, 256)])
+    pick("lvq", "lvs", 0, "l1", "l1s", 0, 256, "lvo", 0, 8)
+    mm("P4", 128, ("lvq", "lvs"), 0, CT, 36)
+    ts(at("dol", 0, 32), at("P4", 0, 32), col(CON), A.add)
+    ts(at("ff", 0, 4), at("rk", 0, 4), 16.0, A.is_lt)
+    pick("dq", "dqs", 0, "l1", "l1s", 0, 256, "dol", 0, 32)
+    nbank = ["P5", "P6", "P7", "P4"]
+    for k in range(4):
+        mm(nbank[k], 128, ("cnq", "cns"), 128 * k, ("lvq", "lvs"), 0)
+        act(at("njk", 0, 16), at(nbank[k], 0, 16), ACT.Copy, acc=at("nsum", k, k + 1))
+    for b in range(4):
+        mm("P%d" % b, 512, EB, 128 * b, ("dq", "dqs"), 0, False, True)
+    act(at("nsg", 0, 4), at("nsum", 0, 4), ACT.Sign, bias=127.5, scale=-1.0)
+    for k in range(4):
+        act(at("nof", k, k + 1), at("nsg", k, k + 1), ACT.Identity, bias=col(MKB + k), scale=64.0)
+    mm("P7", 512, EB, 384, Q, Q0)
+    for c in range(4):
+        ts(at("fmw", c, 512, 4), at("i16", 0, 128), col(TG + c), A.is_equal, at("ff", c, c + 1), A.mult)
+    quant("wq", "ws", 0, 128, "wt", 0)
+    for b in range(4):
+        o, d0, d1 = at("so", 512 * b, 512 * b + 512), at("sm", 0, 512), at("P%d" % b, 0, 512)
+        op("v", lambda: g.vector.tensor_tensor_scan(ap(o), ap(d0), ap(d1), 0.0, A.mult, A.add), [d0, d1], [o])
+        act(at("at", b, 256, 4), at("so", 512 * b + 7, 512 * b + 512, 8), ACT.Copy)
+        if b == 2:
+            cp(at("pol", 0, 4), at("nof", 0, 4))
+    quant("pb", "pbs", 128, 256, "at", 0)
+    pick("pp", "pps", 0, "pb", "pbs", 0, 256, "pol", 0, 4)
+    mm("P4", 128, PP, 0, U, 0)
+    mm("P5", 128, U, 0, PP, 0)
+    act(at("sce2", 64, 65, 1, 0, 64), at("P4", 0, 1, 1, 0, 64), ACT.Abs, bias=TINY)
+    act(at("sce2", 0, 64, 1, 0, 64), at("P5", 0, 64, 1, 0, 64), ACT.Abs, bias=TINY)
+    act(at("tt2", 0, 64, 1, 0, 64), at("lf", 0, 64, 1, 0, 64), ACT.Copy, scale=at("sce2", 64, 65, 1, 0, 64))
+
+    def left(b, bank):
+        tt(at("lft", b, 2048, 4), at("v", b, 2048, 4), at(bank, 0, 512), A.subtract)
+    left(3, "P7")
+    tt(at("cmp2", 0, 64, 1, 0, 64), at("sce2", 0, 64, 1, 0, 64), at("tt2", 0, 64, 1, 0, 64), A.is_gt)
+    ts(col(OB), col(LO), 64.0, A.mult, col(I3), A.add)
+    total(at("rk2", 0, 1, 1, 0, 64), at("cmp2", 0, 64, 1, 0, 64))
+    ts(at("b32", 0, 32), at("b32", 0, 32), col(OB), A.add, float(Q0), A.add)
+    ts(at("oh2", 0, 512, 4, 0, 64), at("i16", 0, 128, 1, 0, 64), at("rk2", 0, 1, 1, 0, 64), A.is_equal)
+    ts(at("oci", 0, 1), at("cf", P_, P_ + 1), 1.0 / WIN, A.mult)
+    quant("ohq", "ohs", 0, 128, "oh2", 0)
+    mm("P6", 128, ("ohq", "ohs"), 0, CT, 68)
+    ts(at("rk2", 1, 2, 1, 0, 64), at("rk2", 0, 1, 1, 0, 64), 16.0, A.is_lt)
+    quant("fwq", "fws", 0, 128, "fmw", 0)
+    ts(at("wol", 0, 1), at("P6", 0, 1), at("P6", 1, 2), A.add)
+    cp(at("nt", 508, 510), at("P6", 0, 2))
+    pick("w2", "w2s", 128, "pp", "pps", 0, 128, "wol", 0, 1)
+    quant("w2", "w2s", 0, 128, "nt", 0)
+
+    for buf, land, f in (("w2", "l2", codes), ("w2s", "l2s", ap)):
+        src, dst = at(buf, 127, 144), at(land, WIN * me, WIN * me + WIN)
+        trs = []
+        for ds, es in ((far, fe), (near, ne)):
+            ids = []
+            for d in ds:
+                rid, pid, _ = topo.addr(d)
+                ids.append(DstId(rid=rid, pnc=pid))
+            trs.append(RemoteDMATransfer(dst_ids=ids, dma_engine_mask=bits(es), remote_sem=T.sem.arr2,
+                                         srcs=[f(src)], dsts=[f(dst) for d in ds]))
+        need("gp", [src], [])
+        g.remote_dma_fused(trs, local_sem=T.sem.lcl)
+        nloc[0] += len(fe) + len(ne)
+        dma("y", f(dst), f(src), [src], [dst])
+    n2 = 0
+    for s in T.cores:
+        if s != core:
+            f2, n2_, e2, ne2 = ways(T, topo, s)
+            n2 += 2 * len(e2 if core in f2 else ne2)
+
+    mm("P7", 128, ("fwq", "fws"), 0, CT, 76)
+    pbank = ["P3", "P4", "P5", "P6"]
+    for b in range(3):
+        mm("P%d" % b, 512, EB, 128 * b, Q, Q0)
+    for b in range(4):
+        mm(pbank[b], 128, EB, 128 * b, PP, 0)
+    tt(at("fo32", 0, 32), at("P7", 0, 32), at("b32", 0, 32), A.add)
+    ts(at("fm", 0, 512, 4, 0, 64), at("i16", 0, 128, 1, 0, 64), col(I_, 0, 64), A.is_equal, at("rk2", 1, 2, 1, 0, 64), A.mult)
+    cp(at("fol", 0, 32), at("fo32", 0, 32))
+    quant("fmq", "fms", 0, 128, "fm", 0)
+    mm("P7", 128, ("fmq", "fms"), 0, CT, 108)
+    for b in range(3):
+        left(b, "P%d" % b)
+    quant("qb", "qs", LEFT + Q0, LEFT + Q0 + 512, "lft", 0)
+    pick("fin", "fis", 0, "qb", "qs", 0, LEFT + Q0 + 512, "fol", 0, 32)
+    dma("y", T.oc[:, 0:2048], codes(at("fin", 0, 512)), [at("fin", 0, 512)], [])
+    for k in range(4):
+        r = at("fis", 0, 512, 1, 32 * k, 32 * k + 4)
+        dma("y", T.osc[4 * k:4 * k + 4, 0:512], ap(r), [at("fis", 0, 512)], [])
+    for b in range(4):
+        tt(at("lpt", b, 512, 4), at("at", b, 512, 4), at(pbank[b], 0, 128), A.subtract)
+    tt(at("go4", 0, 4), at("P7", 0, 4), at("cf", MK, MK + 4), A.add)
+    quant("pp", "pps", 128, 256, "lpt", 0)
+    cp(at("gol", 0, 4), at("go4", 0, 4))
+    cp(col(OC), at("oci", 0, 1))
+    pick("gin", "gis", 0, "pp", "pps", 0, 256, "gol", 0, 4)
+    dma("y", T.oc[:, 2048:2304], codes(at("gin", 0, 64)), [at("gin", 0, 64)], [])
+    for k in range(4):
+        r = at("gis", 0, 64, 1, 32 * k, 32 * k + 4)
+        dma("y", T.osc[4 * k:4 * k + 4, 512:576], ap(r), [at("gis", 0, 64)], [])
+
+    lands("arr2", n2, [at("l2", 0, 136), at("l2s", 0, 136)])
+    mm("P4", 128, ("wq", "ws"), 0, L2, 0)
+    mm("P5", 128, ("wq", "ws"), 0, L2, 8)
+    mm("P6", 128, L2, 0, CT, 112)
+    for o in range(4):
+        cp(at("yo", 16 * o, 16 * o + 16), at("P4", WIN * o + 1, WIN * o + 17))
+        act(at("yo", 64 + 16 * o, 80 + 16 * o), at("P5", WIN * (o + 4) - 7, WIN * (o + 4) + 9), ACT.Copy)
+    dma("y", T.y[:], ap(at("yo", 0, 128)), [at("yo", 0, 128)], [])
+    ts(at("nbs", 0, 16), at("P6", 0, 16), float(N), A.mult, col(OC), A.add)
+    dma("s", T.nb[0:1, 0:128], T.nbs[0:120:17, 0:16], [at("nbs", 0, 16)], [])
+    finish([("lcl", nloc[0])])

@@ -5,59 +5,63 @@ from concourse.mybir import dt, AluOpType, AxisListType, ActivationFunctionType
 CODE = "float8_e4m3fn_x4"
 BFT = "bfloat16"
 F32 = "float32"
-Q0 = 160
-OH1 = Q0 + 512
-LEFT = 704
-BLK = 32
+OH = 192
+Q0 = OH + 264
+V0 = 544
 MSG = 18
-HALF = 112
+OWN = 144
+ZERO = 192
 WIN = 17
+L0 = 15
+HD = 192
+FS = 64
+NEW = FS + 512
 TINY = 2.0 ** -120
+C_DOL, C_WIN, C_FIN, C_NB, C_W, C_END = 12, 76, 80, 112, 128, 264
+Z_X, Z_OH, Z_NUM = 256, 272, 800
 
 SCRATCH = {
-    "ert": ("sbuf", [128, 2048], BFT), "grt": ("sbuf", [128, 2048], BFT), "fz": ("sbuf", [128, 512], BFT),
+    "ert": ("sbuf", [128, 2048], BFT), "grt": ("sbuf", [128, 2048], BFT), "fa": ("sbuf", [128, 512], BFT),
     "uc": ("sbuf", [128, 4], BFT), "ut": ("sbuf", [128, 512], BFT), "wt": ("sbuf", [128, 512], BFT),
-    "ones": ("sbuf", [128, 128], BFT), "idn": ("sbuf", [128, 128], BFT), "eb": ("sbuf", [128, 2048], BFT),
+    "ones": ("sbuf", [128, 128], BFT), "idn": ("sbuf", [128, 128], BFT), "eb": ("sbuf", [128, 516], BFT),
     "ebq": ("sbuf", [128, 512], CODE), "ebs": ("sbuf", [128, 512], "uint8"),
-    "zq": ("sbuf", [128, 128], CODE), "zs": ("sbuf", [128, 128], "uint8"),
-    "ci": ("sbuf", [128, 32], "int32"), "cf": ("sbuf", [128, 112], F32), "z8": ("sbuf", [128, 8], F32),
-    "c64": ("sbuf", [128, 64], F32), "b32": ("sbuf", [128, 32], F32), "lf": ("sbuf", [128, 64], F32),
-    "i16": ("sbuf", [128, 128], BFT), "iadj": ("sbuf", [128, 128], BFT), "sm": ("sbuf", [128, 512], BFT),
-    "ct1": ("sbuf", [128, 544], BFT), "c1q": ("sbuf", [128, 136], CODE), "c1s": ("sbuf", [128, 136], "uint8"),
-    "ct": ("sbuf", [128, 1024], BFT), "ctq": ("sbuf", [128, 256], CODE), "cts": ("sbuf", [128, 256], "uint8"),
-    "cn": ("sbuf", [128, 2048], BFT), "cnq": ("sbuf", [128, 512], CODE), "cns": ("sbuf", [128, 512], "uint8"),
-    "lvo": ("sbuf", [128, 8], "uint16"), "zo": ("sbuf", [128, 4], "uint16"),
+    "ci": ("sbuf", [128, 16], "int32"), "cf": ("sbuf", [128, 96], F32),
+    "c64": ("sbuf", [128, 32], F32), "prm": ("sbuf", [128, 32], F32), "nfin": ("sbuf", [128, 32], F32),
+    "one32": ("sbuf", [128, 128], F32), "lf": ("sbuf", [128, 128], F32), "lf2": ("sbuf", [128, 64], F32),
+    "c4": ("sbuf", [128, 128], BFT), "m12": ("sbuf", [128, 12], F32),
+    "i16": ("sbuf", [128, 144], BFT), "i16d": ("sbuf", [128, 256], BFT), "sm": ("sbuf", [128, 512 - HD], BFT),
+    "ct": ("sbuf", [128, 4 * C_END], BFT), "ctq": ("sbuf", [128, C_END], CODE), "cts": ("sbuf", [128, C_END], "uint8"),
+    "gl": ("sbuf", [128, 8], "uint16"), "lvo": ("sbuf", [128, 8], "uint16"),
     "erq": ("sbuf", [128, 512], CODE), "ers": ("sbuf", [128, 512], "uint8"),
     "uq": ("sbuf", [128, 128], CODE), "us": ("sbuf", [128, 128], "uint8"),
     "wq": ("sbuf", [128, 128], CODE), "ws": ("sbuf", [128, 128], "uint8"),
-    "v": ("sbuf", [128, 2048], BFT), "qb": ("sbuf", [128, 1376], CODE), "qs": ("sbuf", [128, 1376], "uint8"),
-    "sce": ("sbuf", [128, 272], F32), "tt": ("sbuf", [128, 256], F32),
-    "cmp": ("sbuf", [128, 256], F32), "rk": ("sbuf", [128, 4], F32),
-    "oht0": ("sbuf", [128, 528], BFT), "oht1": ("sbuf", [128, 528], BFT),
-    "ol0": ("sbuf", [128, 8], "uint16"), "ol1": ("sbuf", [128, 8], "uint16"),
-    "snd": ("sbuf", [128, 2 * HALF], CODE), "sns": ("sbuf", [128, 2 * HALF], "uint8"),
-    "lft": ("sbuf", [128, 2048], BFT), "ff": ("sbuf", [128, 4], F32), "fmw": ("sbuf", [128, 512], BFT),
-    "fwq": ("sbuf", [128, 128], CODE), "fws": ("sbuf", [128, 128], "uint8"), "fo32": ("sbuf", [128, 32], F32),
-    "fol": ("sbuf", [128, 32], "uint16"), "fin": ("sbuf", [128, 512], CODE), "fis": ("sbuf", [128, 512], "uint8"),
-    "fs": ("sbuf", [128, 2048], BFT), "fsq": ("sbuf", [128, 512], CODE), "fss": ("sbuf", [128, 512], "uint8"),
-    "l1": ("sbuf", [128, 256], CODE), "l1s": ("sbuf", [128, 256], "uint8"),
+    "v": ("sbuf", [128, V0 + 2048], BFT), "qb": ("sbuf", [128, Q0 + 512], CODE), "qs": ("sbuf", [128, Q0 + 512], "uint8"),
+    "zs": ("sbuf", [128, 512], F32), "a2": ("sbuf", [128, 128], F32), "a2t": ("sbuf", [128, 128], F32),
+    "thr": ("sbuf", [128, 256], F32), "cmp": ("sbuf", [128, 256], F32), "junk": ("sbuf", [128, 128], F32),
+    "rk": ("sbuf", [128, 4], F32), "oh1": ("sbuf", [128, 528], BFT),
+    "ol": ("sbuf", [128, 12], "uint16"), "ol4": ("sbuf", [128, 48], "uint16"),
+    "snd": ("sbuf", [128, 192], CODE), "sns": ("sbuf", [128, 192], "uint8"),
+    "vs": ("sbuf", [128, 768], BFT), "lft": ("sbuf", [128, 768], BFT), "val": ("sbuf", [128, 8], F32),
+    "fmw": ("sbuf", [128, 512], BFT), "fwq": ("sbuf", [128, 128], CODE), "fws": ("sbuf", [128, 128], "uint8"),
+    "fo32": ("sbuf", [128, 32], F32), "fol": ("sbuf", [128, 32], "uint16"),
+    "fin": ("sbuf", [128, 576], CODE), "fis": ("sbuf", [128, 576], "uint8"),
+    "fs": ("sbuf", [128, 2048], BFT),
+    "l1": ("sbuf", [128, ZERO + 128], CODE), "l1s": ("sbuf", [128, ZERO + 128], "uint8"),
     "lvq": ("sbuf", [128, 128], CODE), "lvs": ("sbuf", [128, 128], "uint8"),
     "dol": ("sbuf", [128, 32], "uint16"), "dq": ("sbuf", [128, 512], CODE), "dqs": ("sbuf", [128, 512], "uint8"),
-    "so": ("sbuf", [128, 2048], BFT), "at": ("sbuf", [128, 512], BFT),
-    "pb": ("sbuf", [128, 256], CODE), "pbs": ("sbuf", [128, 256], "uint8"),
-    "njk": ("sbuf", [128, 16], F32), "nsum": ("sbuf", [128, 4], F32), "nsg": ("sbuf", [128, 4], F32),
-    "nof": ("sbuf", [128, 4], F32), "pol": ("sbuf", [128, 4], "uint16"),
-    "pp": ("sbuf", [128, 256], CODE), "pps": ("sbuf", [128, 256], "uint8"),
+    "so": ("sbuf", [128, 2048], BFT), "zt": ("sbuf", [128, 804], BFT),
+    "xq": ("sbuf", [128, 132], CODE), "xs": ("sbuf", [128, 132], "uint8"),
+    "pb": ("sbuf", [128, 128], CODE), "pbs": ("sbuf", [128, 128], "uint8"),
+    "po4": ("sbuf", [128, 4], F32), "pol": ("sbuf", [128, 4], "uint16"),
+    "pp": ("sbuf", [128, NEW + 128], CODE), "pps": ("sbuf", [128, NEW + 128], "uint8"),
     "sce2": ("sbuf", [128, 65], F32), "tt2": ("sbuf", [128, 64], F32),
-    "cmp2": ("sbuf", [128, 64], F32), "rk2": ("sbuf", [128, 2], F32), "oh2": ("sbuf", [128, 512], BFT),
+    "cmp2": ("sbuf", [128, 64], F32), "rk2": ("sbuf", [128, 2], F32),
     "ohq": ("sbuf", [128, 128], CODE), "ohs": ("sbuf", [128, 128], "uint8"),
-    "wol": ("sbuf", [128, 2], "uint16"), "nt": ("sbuf", [128, 512], BFT),
+    "wol": ("sbuf", [128, 2], "uint16"), "own": ("sbuf", [128, 2], "uint16"),
     "w2": ("sbuf", [128, 144], CODE), "w2s": ("sbuf", [128, 144], "uint8"),
-    "l2": ("sbuf", [128, 136], CODE), "l2s": ("sbuf", [128, 136], "uint8"),
-    "lpt": ("sbuf", [128, 512], BFT), "fm": ("sbuf", [128, 512], BFT),
-    "fmq": ("sbuf", [128, 128], CODE), "fms": ("sbuf", [128, 128], "uint8"), "go4": ("sbuf", [128, 4], F32),
-    "gol": ("sbuf", [128, 4], "uint16"), "gin": ("sbuf", [128, 64], CODE), "gis": ("sbuf", [128, 64], "uint8"),
-    "oci": ("sbuf", [128, 2], "int32"), "nbs": ("sbuf", [128, 16], F32), "yo": ("sbuf", [128, 128], F32),
+    "l2": ("sbuf", [128, 154], CODE), "l2s": ("sbuf", [128, 154], "uint8"),
+    "go4": ("sbuf", [128, 4], F32), "gol": ("sbuf", [128, 4], "uint16"),
+    "nbs": ("sbuf", [128, 16], F32), "yo": ("sbuf", [128, 128], F32),
 }
 for _k in range(8):
     SCRATCH["P%d" % _k] = ("psum", [128, 512], F32)
@@ -146,21 +150,21 @@ def ways(T, topo, src):
     far = [d for d in T.cores if topo.chip(d) != topo.chip(src)]
     near = [d for d in T.cores if topo.chip(d) == topo.chip(src) and d != src]
     e = topo.engines(src, far[0])
-    return far, near, e, [x for x in topo.engines(src, near[0]) if x not in e][:4]
+    return far, near, e, [x for x in topo.engines(src, near[0]) if x not in e][:2]
 
 
-def plan1(T, topo, src):
-    r = T.rank_of(src)
+def plan1(T, topo, src, half, kind):
     far, near, e, ne = ways(T, topo, src)
-    res = {}
-    for half in (1 - r // 4, r // 4):
-        ds = [d for d in far if T.rank_of(d) // 4 == half]
-        n = len(e) // len(ds)
-        for i, d in enumerate(ds):
-            res[d] = (half, e[n * i:n * i + n])
-    for d in near:
-        res[d] = (T.rank_of(d) // 4, ne)
-    return res
+    ds = [d for d in far if T.rank_of(d) % 2 == half]
+    k = T.rank_of(src) // 2 % len(ds)
+    ds = ds[k:] + ds[:k]
+    n = len(e) // 4
+    e = e[2 * n * kind:] + e[:2 * n * kind]
+    return list(zip(ds, (e[:2 * n], e[2 * n:3 * n], e[3 * n:])))
+
+
+def slot(o, first):
+    return 96 * ((o + first) % 2) + 48 * (o // 4) + (30 if o // 2 % 2 else 0)
 
 
 def bits(es):
@@ -175,8 +179,8 @@ def rank_program(g, core, T, topo):
     ap, need, op, dma, lands, finish = make_flow(g, T)
     A = AluOpType
     ACT = ActivationFunctionType
-    odd, ot = me % 2, me // 2 % 2
-    h0, h1 = 64 * odd, 64 * odd + 64
+    odd, quad = me % 2, me // 2
+    q0, q1 = 32 * quad, 32 * quad + 32
 
     def ts(out, in0, s1, op0, s2=None, op1=None):
         reads = [in0] + [x for x in (s1, s2) if x is not None and not isinstance(x, (int, float))]
@@ -210,6 +214,9 @@ def rank_program(g, core, T, topo):
             kw["accum_out"] = ap(acc)
         op("s", lambda: g.scalar.activation(ap(out), ap(in_), f, **kw), reads, [out] + ([acc] if acc else []))
 
+    def lin(out, in_, scale, bias):
+        act(out, in_, ACT.Identity, bias=bias, scale=scale)
+
     def quant(q, s, a, b, src, c):
         n = b - a
         i = at(src, c, c + 4 * n)
@@ -227,9 +234,13 @@ def rank_program(g, core, T, topo):
            [wq, lst], [oq])
         op("s", lambda: g.scalar.activation(ap(osc), ap(wsc).indirect(ap(lst)), ACT.Copy), [wsc, lst], [osc])
 
-    def zeros(*regions):
-        for name, a, b in regions:
-            act(at(name, a, b), at("eb", 0, b - a), ACT.Copy, scale=0.0)
+    def gather(out, win, lst):
+        op("s", lambda: g.scalar.activation(ap(out), ap(win).indirect(ap(lst)), ACT.Copy), [win, lst], [out])
+
+    def zeros(name, a, b):
+        for c in range(a, b, 512):
+            d = min(b, c + 512)
+            act(at(name, c, d), at("eb", 0, d - c), ACT.Copy, scale=0.0)
 
     def codes(r):
         return ap(r).bitcast(dt.uint8)
@@ -243,355 +254,393 @@ def rank_program(g, core, T, topo):
         else:
             op("gp", lambda: g.iota(ap(out), pattern, base, ch), [], [out])
 
-    def ibit(a, o0, s0, o1=None, s1=None):
-        ts(at("ci", a, a + 4), at("ci", 0, 4), s0, o0, s1, o1)
+    def select(out, in_, pattern, o, fillv, base, ch):
+        op("gp", lambda: g.affine_select(ap(out), ap(in_), pattern, o, fillv, base, ch), [in_], [out])
 
-    def col(a, p0=0, p1=128):
-        return at("cf", a, a + 1, 1, p0, p1)
-    P_, M_, LO, I_, E_, H_, MH, I3 = 0, 4, 8, 12, 16, 20, 24, 28
-    K16, C2, MD, MK, TG, E8, MKM, EV, CON, LVC, M16, MKB, MIDS, OC, OB, HB, MID = \
-        32, 40, 44, 48, 52, 56, 60, 64, 65, 66, 67, 68, 72, 77, 78, 80, 82
-    EB, U, Q, C1, CT, PP, L2 = ("ebq", "ebs"), ("uq", "us"), ("qb", "qs"), ("c1q", "c1s"), ("ctq", "cts"), \
-        ("pp", "pps"), ("l2", "l2s")
+    def col(a, n=1, p0=0, p1=128):
+        return at("cf", a, a + n, 1, p0, p1)
+
+    def whole(*ints):
+        for a, m, s in ints:
+            ts(at("ci", a, a + 1), at("ci", 0, 1), m, A.bitwise_and, s, A.arith_shift_right)
+    P_, K_, A_, I_, B1, H_, S7, MD, E_, O2, KH, M16 = range(12)
+    GL, M3, HI, NB, DL, C0, CON, LVC, BO, X1, X2, BF = range(12, 24)
+    IT4, GP8, K16, TG, LO4, K64, MK, TH4, BM = 24, 32, 40, 44, 48, 52, 60, 64, 68
+    EB, U, Q, CT, PP, L2 = ("ebq", "ebs"), ("uq", "us"), ("qb", "qs"), ("ctq", "cts"), ("pp", "pps"), ("l2", "l2s")
     far, near, fe, ne = ways(T, topo, core)
     nloc = [0]
+    low = 1.0 - 2.0 ** -24
+    first = 1 - odd
+    e0, e1 = slot(me, first) // 32 * 2, (slot(me, first) + MSG + 15) // 16
+    own = OWN + slot(me, first) - 16 * e0
 
     load("y", "ert", 0, 1024, T.er[:, 0:1024])
-    load("s", "ert", 1024, 2048, T.er[:, 1024:2048])
-    load("y", "uc", 0, 4, T.u[:, 0:4])
-    load("y", "grt", 0, 1024, T.gr[:, 0:1024])
-    load("s", "grt", 1024, 2048, T.gr[:, 1024:2048])
-    load("y", "fz", 0, 256, T.fo[:])
+    load("s", "uc", 0, 4, T.u[:, 0:4])
+    load("y", "ert", 1024, 2048, T.er[:, 1024:2048])
+    for a, b in ((0, 1024), (1024, 1536), (1536, 2048)):
+        load("y", "grt", a, b, T.gr[:, a:b])
+    load("y", "fa", 0, 256, T.fo[:])
     load("y", "wt", 0, 512, T.w[:])
 
     fill(at("ones", 0, 128), 1.0)
-    fill(at("oht0", 0, 528), 0.0)
-    op("gp", lambda: g.affine_select(ap(at("idn", 0, 128)), ap(at("ones", 0, 128)), [[-1, 128]], A.is_equal, 0.0, 0, 1),
-       [at("ones", 0, 128)], [at("idn", 0, 128)])
-    iota(at("ci", 0, 4), [[0, 4]], 0, 1)
-    iota(at("c64", 0, 64), [[1, 64]], 0, 0)
-    quant("zq", "zs", 0, 128, "oht0", 0)
-    fill(at("eb", 0, 2048), 0.0)
+    fill(at("eb", 0, 516), 0.0)
+    iota(at("ci", 0, 1), [[0, 1]], 0, 1)
+    select(at("idn", 0, 128), at("ones", 0, 128), [[-1, 128]], A.is_equal, 0.0, 0, 1)
+    fill(at("one32", 0, 128), 1.0)
+    whole((K_, 15, 0), (A_, 127, 5), (I_, 31, 0), (B1, 1, 0), (H_, 127, 6))
+    cp(at("eb", 3, 515, 4), at("idn", 0, 128))
+    zeros("ct", 0, 4 * C_W)
+    cp(at("cf", 0, 6), at("ci", 0, 6))
     for b in range(4):
-        act(at("eb", 512 * b + b, 512 * b + 512, 4), at("idn", 0, 128), ACT.Copy)
-    ibit(M_, A.bitwise_and, 63)
-    ibit(LO, A.bitwise_and, 7)
-    ibit(I_, A.bitwise_and, 15)
-    ibit(E_, A.bitwise_and, 1)
-    ibit(H_, A.arith_shift_right, 6)
-    ibit(MH, A.bitwise_and, 63, A.arith_shift_right, 1)
-    ibit(I3, A.bitwise_and, 15, A.arith_shift_right, 3)
-    quant("ebq", "ebs", 0, 512, "eb", 0)
-    cp(at("cf", 0, 32), at("ci", 0, 32))
-
-    def zslot(o):
-        return BLK * me + (0 if o % 2 else MSG)
-    for buf, land, f in (("zq", "l1", codes), ("zs", "l1s", ap)):
-        src = at(buf, 0, 2)
-        trs = []
-        for ds, es in ((far, fe), (near, ne)):
-            ids, dsts = [], []
-            for d in ds:
-                rid, pid, _ = topo.addr(d)
-                ids.append(DstId(rid=rid, pnc=pid))
-                z = zslot(T.rank_of(d))
-                dsts.append(f(at(land, z, z + 2)))
-            trs.append(RemoteDMATransfer(dst_ids=ids, dma_engine_mask=bits(es), remote_sem=T.sem.arr1,
-                                         srcs=[f(src)], dsts=dsts))
-        need("gp", [src], [])
-        g.remote_dma_fused(trs, local_sem=T.sem.lcl)
-        nloc[0] += len(fe) + len(ne)
-        z = at(land, zslot(me), zslot(me) + 2)
-        dma("y", f(z), f(src), [src], [z])
-    iota(at("iadj", 0, 128, 1, 0, 64), [[0, 8], [1, 16]], 0, 0)
-    iota(at("iadj", 0, 128, 1, 64, 128), [[0, 8], [-1, 16]], 15, 0)
-    iota(at("cf", 40, 44), [[2, 4]], 0, 0)
-    iota(at("cf", 32, 36), [[16, 4]], 0, 0)
-    iota(at("i16", 0, 128), [[0, 8], [1, 16]], 0, 0)
-    iota(at("b32", 0, 32), [[2, 32]], 0, 0)
-    iota(at("ct", 0, 1024), [[0, 1024]], 0, 0)
-    zeros(("ct1", 0, 544), ("oht1", 0, 528))
-    fill(at("z8", 0, 8), 0.0)
-    ts(at("lf", 0, 64), at("c64", 0, 64), col(M_), A.is_lt, -(2.0 ** -24), A.mult)
-    ts(col(EV), col(E_), -1.0, A.mult, 1.0, A.add)
-    tt(col(HB), col(P_), col(I_), A.subtract)
-    ts(at("lf", 0, 64), at("lf", 0, 64), 1.0, A.add)
-    for j, (i, k) in enumerate(((0, -2.0), (1, -1.0), (14, -2.0), (15, -1.0))):
-        ts(col(MIDS + j), col(I_), float(i), A.is_equal, k, A.mult)
-    ts(col(HB + 1), col(HB), 128.0, A.add)
-    for s, b in ((I_, 0), (HB, 32)):
-        act(at("ct1", b + 4, b + 18, 13, 0, 64), at("cf", s, s + 2, 1, 0, 64), ACT.Copy)
-        act(at("ct1", b + 8, b + 22, 13, 64, 128), at("cf", s, s + 2, 1, 64, 128), ACT.Copy)
-    zeros(("fs", 0, 2048), ("cn", 0, 1024))
-
-    quant("erq", "ers", 0, 256, "ert", 0)
-    quant("erq", "ers", 256, 512, "ert", 1024)
-    for b in range(4):
-        mm("P%d" % b, 512, EB, 128 * b, ("erq", "ers"), 0)
+        quant("ebq", "ebs", 128 * b, 128 * b + 128, "eb", 3 - b)
+    for buf, land, f in (("ebq", "l2", codes), ("ebs", "l2s", ap)):
+        src, dst = at(buf, 0, 2), at(land, L0 + N * WIN, L0 + N * WIN + 2)
+        dma("y", f(dst), f(src), [src], [dst])
+    iota(at("m12", 0, 12), [[0, 2], [1, 6]], 0, 0)
+    iota(col(LO4, 2), [[4, 2]], 1, 0)
+    iota(col(BM, 2), [[-388, 2]], -1, 0)
+    iota(col(GP8, 8), [[256, 2], [4, 2], [128, 2]], 0, 0)
+    iota(at("i16d", 0, 256), [[0, 8], [1, 16], [0, 2]], 0, 0)
+    for a in range(4):
+        select(at("lf", 0, 128, 1, 32 * a, 32 * a + 32), at("one32", 0, 128, 1, 32 * a, 32 * a + 32),
+               [[1, 2], [-1, 2], [-2, 32]], A.is_gt, low, 0, 2)
+    iota(at("fs", 1536, 2048), [[0, 512]], 0, 0)
+    iota(at("c64", 0, 32), [[1, 32]], 0, 0)
+    iota(at("prm", 0, 32), [[4, 2], [8, 4], [1, 4]], 0, 0)
+    iota(at("c4", 0, 128), [[1, 32], [0, 4]], 0, 0)
+    iota(at("i16", 0, 144), [[0, 9], [1, 16]], 0, 0)
+    iota(col(K16, 4), [[16, 4]], 0, 0)
+    ts(col(M3), col(A_), 2.0, A.mult, col(H_), A.subtract)
+    ts(col(NB), col(B1), -8.0, A.mult, col(A_), A.add)
+    ts(col(HI), col(I_), col(B1), A.add, 8.0, A.mult)
+    ts(at("m12", 0, 12), at("m12", 0, 12), col(M3), A.is_equal)
+    ts(col(LO4, 2), col(LO4, 2), col(NB), A.add)
+    ts(col(GL), col(K_), 8.0, A.mult, col(A_), A.add)
+    ts(col(BM, 2), col(BM, 2), col(B1), A.add)
+    ts(at("gl", 0, 8), col(GP8, 8), col(GL), A.add)
+    zeros("v", 512, V0)
+    zeros("oh1", 512, 528)
     for t in range(4):
-        ts(at("ut", t, 512, 4), at("ones", 0, 128), at("uc", t, t + 1), A.mult)
-    total(col(MID), at("cf", MIDS, MIDS + 4))
+        lin(at("ut", t, 512, 4), at("ones", 0, 128), 0.0, at("uc", t, t + 1))
+    for b in range(2):
+        act(at("ct", b, 48, 4), at("m12", 0, 12), ACT.Copy, scale=col(LO4 + b))
+        act(at("ct", 2 + b, 48, 4), at("m12", 0, 12), ACT.Copy, scale=col(HI))
+    for t in range(2):
+        lin(at("ct", 4 + t, 48, 12, 0, 32), at("ones", 0, 4, 1, 0, 32), 0.0, -448.0)
+    zeros("fs", 0, 1536)
+
+    def unpack(i):
+        quant("erq", "ers", 256 * i, 256 * i + 256, "ert", 1024 * i)
+        for k in range(4):
+            mm("P%d" % (4 * i + k), 256, EB, 128 * k, ("erq", "ers"), 256 * i)
+
+    def vadd(a, b, h, *ks):
+        c, i, h = V0 + 1024 * h, a // 256, (h + first) % 2
+        for k in ks or range(4):
+            tt(at("v", c + 2 * a + k, c + 2 * b, 4), at("P%d" % (4 * i + k), h + a - 256 * i, b - 256 * i, 2),
+               at("grt", 4 * (a + h) + k, 4 * b, 8), A.add)
+
+    def packed(a, b):
+        quant("qb", "qs", Q0 + a, Q0 + b, "v", V0 + 4 * a)
+
+    def scored(a, b, bk):
+        mm(bk, b - a, U, 0, Q, Q0 + a)
+        act(at("zs", a, b), at(bk, 0, b - a), ACT.Abs, bias=TINY)
+
+    unpack(0)
     quant("uq", "us", 0, 128, "ut", 0)
-    quant("c1q", "c1s", 0, 136, "ct1", 0)
-    ts(at("ol0", 0, 7, 3), at("z8", 0, 3), col(MID), A.add, 130.0, A.add)
-    ts(at("ol1", 0, 7, 3), at("z8", 0, 3), col(MID), A.add, float(OH1 - Q0 - 256 + 130), A.add)
+    unpack(1)
+    quant("ctq", "cts", 0, C_W, "ct", 0)
+    vadd(0, 256, 0)
+    vadd(0, 256, 1, 0)
+    packed(0, 128)
+    for k in range(4):
+        vadd(256, 384, 0, k)
+        vadd(384, 512, 0, k)
+        if k < 3:
+            vadd(0, 256, 1, k + 1)
+    scored(0, 128, "P0")
+    packed(128, 256)
+    scored(128, 256, "P1")
+    packed(256, 384)
+    vadd(256, 512, 1)
 
-    def vadd(b, *owners):
-        for o in owners:
-            tt(at("v", 256 * o + b, 256 * o + 256, 4), at("P%d" % b, o, 512, N), at("grt", 4 * o + b, 2048, 4 * N), A.add)
+    OHT = ("v", "oh1")
+    LB = ("P6", "P7")
 
-    def scored(c, p1, p2):
-        a, k = Q0 + 128 * c, 68 * c
-        quant("qb", "qs", a, a + 128, "v", 512 * c)
-        mm(p1, 128, Q, a, U, 0)
-        mm(p2, 128, U, 0, Q, a)
-        act(at("sce", k + 64, k + 65), at(p1, 0, 1), ACT.Abs, bias=TINY)
-        act(at("sce", k, k + 64, 1, 0, 64), at(p2, 0, 64, 1, 0, 64), ACT.Abs, bias=TINY)
-        act(at("sce", k, k + 64, 1, 64, 128), at(p2, 64, 128, 1, 64, 128), ACT.Abs, bias=TINY)
-        act(at("tt", 64 * c, 64 * c + 64), at("lf", 0, 64), ACT.Copy, scale=at("sce", k + 64, k + 65))
+    def turned(h):
+        o, i = at("a2t", 64 * h, 64 * h + 64), at("a2", 64 * h, 64 * h + 64)
+        op("v", lambda: g.vector.transpose(ap(o), ap(i)), [i], [o])
+
+    def limit(c):
+        b, h = c // 2, c % 2
+        tt(at("thr", 64 * c, 64 * c + 64), at("a2", 64 * h, 64 * h + 64), at("lf", 64 * b, 64 * b + 64), A.mult)
 
     def beats(c):
-        tt(at("cmp", 64 * c, 64 * c + 64), at("sce", 68 * c, 68 * c + 64), at("tt", 64 * c, 64 * c + 64), A.is_gt)
+        a = 64 * (c % 2) + 32 * (c // 2)
+        ts(at("cmp", 64 * c, 64 * c + 64), at("thr", 64 * c, 64 * c + 64), at("a2t", a, a + 1), A.is_ge)
 
-    def ranks(c):
-        total(at("rk", c, c + 1), at("cmp", 64 * c, 64 * c + 64))
+    def count(c):
+        if c % 2:
+            act(at("junk", 32 * c - 32, 32 * c + 32), at("cmp", 64 * c, 64 * c + 64), ACT.Copy, acc=at("rk", c, c + 1))
+        else:
+            total(at("rk", c, c + 1), at("cmp", 64 * c, 64 * c + 64))
 
     def onehot(c):
-        ts(at("oht%d" % (c // 2), c % 2, 512, 4), at("iadj", 0, 128), at("rk", c, c + 1), A.is_equal)
+        ts(at(OHT[c % 2], c // 2, 512, 2), at("i16d", 0, 256), at("rk", c, c + 1), A.is_equal)
 
-    def listed(h, bank):
-        oh, r = "oht%d" % h, at("rk", 2 * h, 2 * h + 2)
-        ts(at(oh, 512, 514), r, 16.0, A.min, col(EV), A.mult)
-        ts(at(oh, 516, 518), r, 16.0, A.min, col(E_), A.mult)
-        a = OH1 * h
-        quant("qb", "qs", a, a + 132, oh, 0)
-        mm(bank, 128, Q, a, C1, 0, True, False)
-        mm(bank, 128, Q, a, C1, 8, False, True)
+    def rankcols(h):
+        cp(at(OHT[h], 520, 528, 4), at("rk", h, 4, 2))
+        act(at(OHT[h], 521, 528, 4), at("rk", h, 4, 2), ACT.Relu, bias=-15.0)
 
-    def offsets(h, bank):
-        for j in (1, 4):
-            ts(at("ol%d" % h, j, j + 2), at(bank, j, j + 2), 0.0 if h else float(Q0), A.add)
+    def listed(h):
+        a = OH + 132 * (1 - h)
+        quant("qb", "qs", a, a + 132, OHT[h], 0)
+        mm(LB[h], 128, Q, a, CT, 0)
+
+    def offsets(h):
+        ts(at("ol", 6 * h, 6 * h + 6), at(LB[h], 6 * h, 6 * h + 6), col(BM + h), A.max, float(Q0 - OH - 1 + 256 * h), A.add)
 
     def picked(h):
-        a, b = (Q0 + 256, OH1 + 132) if h else (0, Q0 + 256)
-        pick("snd", "sns", HALF * h, "qb", "qs", a, b, "ol%d" % h, 0, 7)
+        pick("snd", "sns", 96 * h, "qb", "qs", OH, Q0 + 256 * (1 + h), "ol", 6 * h, 6 * h + 6)
 
-    def slot(o):
-        return HALF * (o // 4) + 48 * (o // 2 % 2) + (32 if o % 2 else 14)
-
-    def lslot(o):
-        return BLK * me + (2 if o % 2 else 0)
-    plan = plan1(T, topo, core)
-
-    def sent(half):
-        for buf, land, f in (("snd", "l1", codes), ("sns", "l1s", ap)):
+    def sent(h):
+        for kind, (buf, land, f) in enumerate((("snd", "l1", codes), ("sns", "l1s", ap))):
             trs, rs = [], []
-            for d in plan:
-                if plan[d][0] == half:
-                    o = T.rank_of(d)
-                    r, l = at(buf, slot(o), slot(o) + MSG), at(land, lslot(o), lslot(o) + MSG)
-                    rid, pid, _ = topo.addr(d)
-                    trs.append(RemoteDMATransfer(dst_ids=[DstId(rid=rid, pnc=pid)], dma_engine_mask=bits(plan[d][1]),
-                                                 remote_sem=T.sem.arr1, src=f(r), dst=f(l)))
-                    rs.append(r)
-                    nloc[0] += len(plan[d][1])
+            for d, es in plan1(T, topo, core, (h + first) % 2, kind) + [(near[0], ne)] * (h != kind):
+                o = T.rank_of(d)
+                r, l = at(buf, slot(o, first), slot(o, first) + MSG), at(land, MSG * me, MSG * me + MSG)
+                rid, pid, _ = topo.addr(d)
+                trs.append(RemoteDMATransfer(dst_ids=[DstId(rid=rid, pnc=pid)], dma_engine_mask=bits(es),
+                                             remote_sem=T.sem.arr1, src=f(r), dst=f(l)))
+                rs.append(r)
+                nloc[0] += len(es)
             need("gp", rs, [])
             g.remote_dma_fused(trs, local_sem=T.sem.lcl)
 
-    first, second = 1 - me // 4, me // 4
-    cA, cB, cC, cD = 2 * first, 2 * first + 1, 2 * second, 2 * second + 1
-    of, os_ = range(4 * first, 4 * first + 4), range(4 * second, 4 * second + 4)
-    for b in range(3):
-        vadd(b, *of)
-    vadd(0, *os_)
-    vadd(3, 2 * cA, 2 * cA + 1)
-    scored(cA, "P4", "P5")
-    vadd(3, 2 * cB, 2 * cB + 1)
-    scored(cB, "P6", "P7")
-    vadd(1, *os_)
-    vadd(2, *os_)
-    beats(cA)
-    vadd(3, 2 * cC)
-    beats(cB)
-    ranks(cA)
-    vadd(3, 2 * cC + 1)
-    ranks(cB)
-    onehot(cA)
-    scored(cC, "P4", "P5")
-    onehot(cB)
-    listed(first, "P0")
-    vadd(3, 2 * cD, 2 * cD + 1)
-    scored(cD, "P6", "P7")
-    beats(cC)
-    offsets(first, "P0")
-    ranks(cC)
-    picked(first)
-    sent(first)
-    onehot(cC)
-    beats(cD)
-    ranks(cD)
-    onehot(cD)
-    listed(second, "P1")
-    ts(at("cf", MKM, MKM + 4), at("cf", K16, K16 + 4), -1.0, A.mult, col(M_), A.add)
-    tt(at("cf", MD, MD + 4), at("cf", M_, M_ + 4), at("cf", LO, LO + 4), A.subtract)
-    tt(col(M16), col(M_), col(I_), A.subtract)
-    ts(col(CON), col(LO), float(BLK), A.mult, 17.0 if odd else 2.0, A.add)
-    ts(col(LVC), col(LO), float(BLK), A.mult, col(I3), A.add)
-    offsets(second, "P1")
-    ts(col(E8), col(E_), 8.0, A.mult)
-    ts(at("lvo", 0, 8), at("z8", 0, 8), col(LVC), A.add, 18.0 if odd else 0.0, A.add)
-    picked(second)
-    ts(at("cf", TG, TG + 4), at("cf", C2, C2 + 4), col(H_), A.add, col(E8), A.add)
-    sent(second)
-    mine, mine_s = at("snd", slot(me), slot(me) + MSG), at("sns", slot(me), slot(me) + MSG)
-    home, home_s = at("l1", lslot(me), lslot(me) + MSG), at("l1s", lslot(me), lslot(me) + MSG)
-    dma("y", codes(home), codes(mine), [mine], [home])
-    dma("y", ap(home_s), ap(mine_s), [mine_s], [home_s])
-    n1 = 0
-    for s in T.cores:
-        if s != core:
-            f2, n2_, e2, ne2 = ways(T, topo, s)
-            n1 += 2 * len(plan1(T, topo, s)[core][1]) + 2 * len(e2 if core in f2 else ne2)
-
-    zeros(("cn", 1024, 2048), ("fz", 256, 512))
+    gather(at("a2", 0, 64), at("zs", 0, 256), at("gl", 0, 4))
+    scored(256, 384, "P2")
+    packed(384, 512)
+    scored(384, 512, "P3")
+    gather(at("a2", 64, 128), at("zs", 0, 512), at("gl", 4, 8))
+    limit(0)
+    turned(0)
+    limit(2)
+    beats(0)
+    beats(2)
+    count(0)
+    count(2)
+    onehot(0)
+    onehot(2)
+    rankcols(0)
+    turned(1)
+    listed(0)
+    limit(1)
+    limit(3)
+    offsets(0)
+    beats(1)
+    picked(0)
+    sent(0)
+    count(1)
+    beats(3)
+    count(3)
+    whole((S7, 7, 0), (MD, 56, 0))
+    onehot(1)
+    onehot(3)
+    rankcols(1)
     for b in range(4):
-        act(at("fs", b, 2048, 32), at("fz", b, 256, 4), ACT.Copy)
-    act(at("sm", 0, 512), at("eb", 0, 512), ACT.Identity, bias=1.0, scale=0.0)
-    act(at("sm", 0, 512, 8), at("eb", 0, 64), ACT.Copy, scale=0.0)
-    for name, a, b in (("at", 256, 512), ("oh2", 0, 512), ("nt", 0, 512), ("fm", 0, 512)):
-        iota(at(name, a, b), [[0, b - a]], 0, 0)
-    ts(at("ct", 144 + ot, 144 + 128, 4, h0, h1), at("c64", 0, 32, 1, h0, h1), col(MH, h0, h1), A.is_equal,
-       -1.0 if odd else 1.0, A.mult)
-    cp(at("ct", 276, 277, 1, 0, 64), at("cf", LO, LO + 1, 1, 0, 64))
-    cp(at("ct", 272, 273, 1, 0, 64), at("cf", MD, MD + 1, 1, 0, 64))
+        act(at("fs", b, 2048, 32), at("fa", b, 256, 4), ACT.Copy)
+    listed(1)
+    whole((E_, 15, 3), (O2, 7, 2), (KH, 15, 1))
+    offsets(1)
+    whole((M16, 48, 0))
+    picked(1)
+    sent(1)
+    iota(col(IT4, 4), [[8, 2], [1 - 2 * first, 2]], first, 0)
+    iota(col(K64, 4), [[16, 4]], 64, 0)
+    iota(at("nfin", 0, 32), [[8, 32]], Q0, 0)
+    select(at("lf2", 0, 64, 1, 0, 64), at("one32", 0, 64, 1, 0, 64), [[-1, 64]], A.is_gt, low, 0, 1)
+    n1 = sum(len(es) for s in T.cores if s != core for kind in range(2)
+             for d, es in plan1(T, topo, s, odd, kind) if d == core) + 2 * len(ne)
+
+    def part(h):
+        return (HD, 512) if h else (0, HD)
+
+    def start(b, h):
+        a, c = part(h)
+        mm("P%d" % (4 * h + b), c - a, EB, 128 * b, PP, FS + a, True, False)
     for t in range(4):
-        ts(at("ct", 304 + t, 304 + 128, 4), at("c64", 0, 32), col(MH), A.is_equal, float(LEFT), A.mult)
-    ts(at("ct", 432, 448, 4, 0, 64), at("cf", K16, K16 + 4, 1, 0, 64), col(M16, 0, 64), A.is_equal, 128.0, A.mult)
-    for t in range(2):
-        ts(at("ct", 448 + t, 448 + 64, 4), at("c64", 0, 16), col(P_), A.is_equal)
-    quant("ctq", "cts", 0, 256, "ct", 0)
-    ts(at("cf", MK, MK + 4), at("cf", K16, K16 + 4), col(I_), A.add)
-    ts(at("cf", MKB, MKB + 4), at("cf", K16, K16 + 4), col(I_), A.add, 64.0, A.add)
-    ts(at("zo", 0, 4), at("z8", 0, 4), 64.0, A.add)
-    quant("pb", "pbs", 0, 128, "fz", 0)
-    quant("fsq", "fss", 0, 512, "fs", 0)
-    for b in range(4):
-        mm("P%d" % b, 512, EB, 128 * b, ("fsq", "fss"), 0, True, False)
-    for k in range(4):
-        ts(at("cn", 512 * k + ot, 512 * k + 512, 4, h0, h1), at("i16", 0, 128, 1, h0, h1), col(MKM + k, h0, h1), A.is_equal)
-    pick("pp", "pps", 64, "pb", "pbs", 0, 128, "zo", 0, 4)
-    quant("cnq", "cns", 0, 512, "cn", 0)
+        ts(at("ol4", 12 * t, 12 * t + 12), at("ol", 0, 12), 4.0, A.mult, float(V0 - 4 * (Q0 - OH) + t), A.add)
+    for t in range(4):
+        gather(at("vs", 192 * t, 192 * t + 192), at("v", 0, V0 + 2048), at("ol4", 12 * t, 12 * t + 12))
+    quant("pp", "pps", FS, NEW, "fs", 0)
+    for b in range(7):
+        start(b % 4, b // 4)
+    cp(at("cf", 6, 12), at("ci", 6, 12))
+    fill(at("zt", Z_X, Z_NUM + 4), 0.0)
+    ts(col(DL), col(S7), float(me), A.is_equal, float(own - MSG * me), A.mult)
+    pick("l1", "l1s", OWN, "qb", "qs", OH, Q0 + 512, "ol", e0, e1)
+    quant("l1", "l1s", ZERO, ZERO + 128, "zt", Z_OH)
+    ts(col(C0), col(S7), float(MSG), A.mult, col(DL), A.add)
+    lin(col(CON), col(C0), 1.0, 2.0 if quad % 2 else 0.0)
+    lin(at("zt", Z_OH, Z_OH + 16, 4, 32, 64), col(K16, 4, 32, 64), 0.5, 0.0)
+    lin(col(MK, 4), col(K16, 4), 1.0, col(K_))
+    lin(col(BF), col(B1), 1.0 - 2 * first, float(first))
+    lin(col(X1), col(B1), -1.0, col(S7))
+    lin(col(X2), col(BF), 256.0, col(KH))
+    ts(col(LVC), col(C0), col(E_), A.add, 0.0 if quad % 2 else 16.0, A.add)
+    for t, c in ((0, 1.0), (1, 256.0)):
+        for a, src in ((4 * C_DOL, "c64"), (4 * C_DOL + 128, "prm")):
+            ts(at("ct", a + t, a + 128, 4, q0, q1), at(src, 0, 32, 1, q0, q1), col(I_, 1, q0, q1), A.is_equal, c, A.mult)
+    ts(at("lvo", 0, 8), at("c64", 0, 8), 0.0, A.mult, col(LVC), A.add)
+    ts(at("ct", 4 * C_FIN, 4 * C_FIN + 128), at("c4", 0, 128), col(I_), A.is_equal)
+    ts(at("ct", 4 * C_NB, 4 * C_NB + 64), at("c4", 0, 64), col(P_), A.is_equal)
+    cp(at("ct", 4 * C_WIN, 4 * C_WIN + 8, 4, 0, 64), col(S7, 2, 0, 64))
+    fill(at("sm", 0, 512 - HD), 1.0)
+    quant("ctq", "cts", 0, C_W, "ct", 0)
+    fill(at("sm", 0, 512 - HD, 8), 0.0)
+    fill(at("ct", 4 * C_W, 4 * C_END, 1, 0, 64), 0.0)
+    for t in range(4):
+        ts(at("ct", 4 * C_W + t, 4 * C_END, 4, 64, 128), at("i16", 0, 136, 1, 64, 128), 2.0 * t, A.subtract,
+           col(E_, 1, 64, 128), A.is_equal)
+    ts(at("ct", 4 * C_W, 4 * C_W + 512, 4, 0, 64), at("i16", 0, 128, 1, 0, 64), col(K_, 1, 0, 64), A.is_equal)
+    fill(at("zt", Z_NUM + 2, Z_NUM + 3), float(me))
+    quant("ctq", "cts", C_W, C_END, "ct", 4 * C_W)
 
-    lands("arr1", n1, [at("l1", 0, 256), at("l1s", 0, 256)])
-    pick("lvq", "lvs", 0, "l1", "l1s", 0, 256, "lvo", 0, 8)
-    mm("P4", 128, ("lvq", "lvs"), 0, CT, 36)
-    ts(at("dol", 0, 32), at("P4", 0, 32), col(CON), A.add)
-    ts(at("ff", 0, 4), at("rk", 0, 4), 16.0, A.is_lt)
-    pick("dq", "dqs", 0, "l1", "l1s", 0, 256, "dol", 0, 32)
-    nbank = ["P5", "P6", "P7", "P4"]
-    for k in range(4):
-        mm(nbank[k], 128, ("cnq", "cns"), 128 * k, ("lvq", "lvs"), 0)
-        act(at("njk", 0, 16), at(nbank[k], 0, 16), ACT.Copy, acc=at("nsum", k, k + 1))
-    for b in range(4):
-        mm("P%d" % b, 512, EB, 128 * b, ("dq", "dqs"), 0, False, True)
-    act(at("nsg", 0, 4), at("nsum", 0, 4), ACT.Sign, bias=127.5, scale=-1.0)
-    for k in range(4):
-        act(at("nof", k, k + 1), at("nsg", k, k + 1), ACT.Identity, bias=col(MKB + k), scale=64.0)
-    mm("P7", 512, EB, 384, Q, Q0)
-    for c in range(4):
-        ts(at("fmw", c, 512, 4), at("i16", 0, 128), col(TG + c), A.is_equal, at("ff", c, c + 1), A.mult)
-    quant("wq", "ws", 0, 128, "wt", 0)
-    for b in range(4):
-        o, d0, d1 = at("so", 512 * b, 512 * b + 512), at("sm", 0, 512), at("P%d" % b, 0, 512)
+    lands("arr1", n1, [at("l1", 0, OWN), at("l1s", 0, OWN)])
+    pick("lvq", "lvs", 0, "l1", "l1s", 0, ZERO + 128, "lvo", 0, 8)
+    mm("P7", 128, ("lvq", "lvs"), 0, CT, 0)
+    ts(at("val", 4, 8), at("rk", 0, 4), 16.0, A.is_ge, 1024.0, A.mult)
+    ts(col(TG, 4), col(IT4, 4), col(A_), A.add, col(A_), A.add)
+    tt(at("val", 0, 4), at("val", 4, 8), at("rk", 0, 4), A.max)
+    ts(col(X1), col(X1), col(O2), A.subtract, 16.0, A.mult)
+    ts(at("dol", 0, 32), at("P7", C_DOL, C_DOL + 32), col(CON), A.add, float(ZERO), A.min)
+    DQ = ("dq", "dqs")
+
+    def dense(b, h):
+        a, c = part(h)
+        mm("P%d" % (4 * h + b), c - a, EB, 128 * b, DQ, a, False, True)
+
+    def scan(b, h):
+        a, c = part(h)
+        o, d0, d1 = at("so", 512 * b + a, 512 * b + c), at("sm", 0, c - a), at("P%d" % (4 * h + b), 0, c - a)
         op("v", lambda: g.vector.tensor_tensor_scan(ap(o), ap(d0), ap(d1), 0.0, A.mult, A.add), [d0, d1], [o])
-        act(at("at", b, 256, 4), at("so", 512 * b + 7, 512 * b + 512, 8), ACT.Copy)
-        if b == 2:
-            cp(at("pol", 0, 4), at("nof", 0, 4))
-    quant("pb", "pbs", 128, 256, "at", 0)
-    pick("pp", "pps", 0, "pb", "pbs", 0, 256, "pol", 0, 4)
-    mm("P4", 128, PP, 0, U, 0)
+        if h and b < 3:
+            act(at("fa", 256 + b, 512, 4), at("so", 512 * b + 7, 512 * b + 512, 8), ACT.Copy)
+    ts(at("zt", Z_OH, Z_OH + 32, 1, 64, 128), at("P7", C_DOL + 32, C_DOL + 64, 1, 64, 128), 16.0, A.is_lt, 64.0, A.mult)
+    start(3, 1)
+    pick("dq", "dqs", 0, "l1", "l1s", 0, ZERO + 128, "dol", 0, HD // 16)
+    for b in range(4):
+        dense(b, 0)
+    pick("dq", "dqs", HD, "l1", "l1s", 0, ZERO + 128, "dol", HD // 16, 32)
+    for b in range(4):
+        dense(b, 1)
+    for b in range(4):
+        scan(b, 0)
+    quant("xq", "xs", 0, 132, "zt", Z_OH)
+    mm("P0", 128, CT, C_W, ("xq", "xs"), 0, True, False)
+    mm("P0", 128, CT, C_W + 8, ("xq", "xs"), 4, False, True)
+    for b in range(4):
+        scan(b, 1)
+    tt(at("po4", 0, 4), at("P0", 0, 4), col(K64, 4), A.min)
+    cp(at("fa", 259, 512, 4), at("so", 1543, 2048, 8))
+    ts(at("pol", 0, 4), at("po4", 0, 4), col(K_), A.add)
+    quant("pb", "pbs", 0, 128, "fa", 0)
+    pick("pp", "pps", 0, "pb", "pbs", 0, 128, "pol", 0, 4)
+
+    def rest(b):
+        mm("P%d" % b, 192, EB, 128 * b, ("snd", "sns"), 0)
+
+    def left(b):
+        tt(at("lft", b, 768, 4), at("vs", 192 * b, 192 * b + 192), at("P%d" % b, 0, 192), A.subtract)
+
+    def kept(t):
+        ts(at("fmw", t, 512, 4), at("i16", 0, 128), col(TG + t), A.is_equal, at("val", t, t + 1), A.mult)
+    rest(1)
     mm("P5", 128, U, 0, PP, 0)
-    act(at("sce2", 64, 65, 1, 0, 64), at("P4", 0, 1, 1, 0, 64), ACT.Abs, bias=TINY)
+    mm("P4", 128, PP, 0, U, 0)
     act(at("sce2", 0, 64, 1, 0, 64), at("P5", 0, 64, 1, 0, 64), ACT.Abs, bias=TINY)
-    act(at("tt2", 0, 64, 1, 0, 64), at("lf", 0, 64, 1, 0, 64), ACT.Copy, scale=at("sce2", 64, 65, 1, 0, 64))
-
-    def left(b, bank):
-        tt(at("lft", b, 2048, 4), at("v", b, 2048, 4), at(bank, 0, 512), A.subtract)
-    left(3, "P7")
-    tt(at("cmp2", 0, 64, 1, 0, 64), at("sce2", 0, 64, 1, 0, 64), at("tt2", 0, 64, 1, 0, 64), A.is_gt)
-    ts(col(OB), col(LO), 64.0, A.mult, col(I3), A.add)
+    act(at("sce2", 64, 65, 1, 0, 64), at("P4", 0, 1, 1, 0, 64), ACT.Abs, bias=TINY)
+    rest(0)
+    rest(2)
+    left(1)
+    lin(col(BO), col(BF), 96.0, col(X1))
+    for t in range(3):
+        kept(t)
+    tt(at("tt2", 0, 64, 1, 0, 64), at("sce2", 0, 64, 1, 0, 64), at("lf2", 0, 64, 1, 0, 64), A.mult)
+    ts(at("cmp2", 0, 64, 1, 0, 64), at("tt2", 0, 64, 1, 0, 64), at("sce2", 64, 65, 1, 0, 64), A.is_ge)
     total(at("rk2", 0, 1, 1, 0, 64), at("cmp2", 0, 64, 1, 0, 64))
-    ts(at("b32", 0, 32), at("b32", 0, 32), col(OB), A.add, float(Q0), A.add)
-    ts(at("oh2", 0, 512, 4, 0, 64), at("i16", 0, 128, 1, 0, 64), at("rk2", 0, 1, 1, 0, 64), A.is_equal)
-    ts(at("oci", 0, 1), at("cf", P_, P_ + 1), 1.0 / WIN, A.mult)
-    quant("ohq", "ohs", 0, 128, "oh2", 0)
-    mm("P6", 128, ("ohq", "ohs"), 0, CT, 68)
-    ts(at("rk2", 1, 2, 1, 0, 64), at("rk2", 0, 1, 1, 0, 64), 16.0, A.is_lt)
-    quant("fwq", "fws", 0, 128, "fmw", 0)
-    ts(at("wol", 0, 1), at("P6", 0, 1), at("P6", 1, 2), A.add)
-    cp(at("nt", 508, 510), at("P6", 0, 2))
+    ts(at("zt", Z_OH, Z_OH + 512, 4, 0, 64), at("i16", 0, 128, 1, 0, 64), at("rk2", 0, 1, 1, 0, 64), A.is_equal)
+    quant("ohq", "ohs", 0, 128, "zt", Z_OH)
+    mm("P6", 128, ("ohq", "ohs"), 0, CT, 0)
+    rest(3)
+    left(0)
+    kept(3)
+    ts(at("zt", Z_NUM, Z_NUM + 2), at("P6", C_WIN, C_WIN + 2), float(N), A.mult)
+    ts(at("wol", 0, 1), at("P6", C_WIN, C_WIN + 1), at("P6", C_WIN + 1, C_WIN + 2), A.add)
+    quant("w2", "w2s", 0, 128, "zt", Z_NUM + 4 - 512)
     pick("w2", "w2s", 128, "pp", "pps", 0, 128, "wol", 0, 1)
-    quant("w2", "w2s", 0, 128, "nt", 0)
 
+    def home(land, o, d):
+        a = L0 + WIN * ((o - d) % N)
+        return at(land, a, a + WIN)
     for buf, land, f in (("w2", "l2", codes), ("w2s", "l2s", ap)):
-        src, dst = at(buf, 127, 144), at(land, WIN * me, WIN * me + WIN)
+        src = at(buf, 127, 144)
         trs = []
-        for ds, es in ((far, fe), (near, ne)):
-            ids = []
-            for d in ds:
-                rid, pid, _ = topo.addr(d)
-                ids.append(DstId(rid=rid, pnc=pid))
-            trs.append(RemoteDMATransfer(dst_ids=ids, dma_engine_mask=bits(es), remote_sem=T.sem.arr2,
-                                         srcs=[f(src)], dsts=[f(dst) for d in ds]))
+        k = 2 * (quad % 3)
+        for ds, es in ((far[k:] + far[:k], fe), (near, ne)):
+            ids = [DstId(rid=topo.addr(d)[0], pnc=topo.addr(d)[1]) for d in ds]
+            trs.append(RemoteDMATransfer(dst_ids=ids, dma_engine_mask=bits(es), remote_sem=T.sem.arr2, srcs=[f(src)],
+                                         dsts=[f(home(land, me, T.rank_of(d))) for d in ds]))
         need("gp", [src], [])
         g.remote_dma_fused(trs, local_sem=T.sem.lcl)
         nloc[0] += len(fe) + len(ne)
-        dma("y", f(dst), f(src), [src], [dst])
-    n2 = 0
-    for s in T.cores:
-        if s != core:
-            f2, n2_, e2, ne2 = ways(T, topo, s)
-            n2 += 2 * len(e2 if core in f2 else ne2)
 
-    mm("P7", 128, ("fwq", "fws"), 0, CT, 76)
-    pbank = ["P3", "P4", "P5", "P6"]
-    for b in range(3):
-        mm("P%d" % b, 512, EB, 128 * b, Q, Q0)
+    quant("fwq", "fws", 0, 128, "fmw", 0)
+    mm("P1", 128, ("fwq", "fws"), 0, CT, 0)
     for b in range(4):
-        mm(pbank[b], 128, EB, 128 * b, PP, 0)
-    tt(at("fo32", 0, 32), at("P7", 0, 32), at("b32", 0, 32), A.add)
-    ts(at("fm", 0, 512, 4, 0, 64), at("i16", 0, 128, 1, 0, 64), col(I_, 0, 64), A.is_equal, at("rk2", 1, 2, 1, 0, 64), A.mult)
-    cp(at("fol", 0, 32), at("fo32", 0, 32))
-    quant("fmq", "fms", 0, 128, "fm", 0)
-    mm("P7", 128, ("fmq", "fms"), 0, CT, 108)
-    for b in range(3):
-        left(b, "P%d" % b)
-    quant("qb", "qs", LEFT + Q0, LEFT + Q0 + 512, "lft", 0)
-    pick("fin", "fis", 0, "qb", "qs", 0, LEFT + Q0 + 512, "fol", 0, 32)
-    dma("y", T.oc[:, 0:2048], codes(at("fin", 0, 512)), [at("fin", 0, 512)], [])
-    for k in range(4):
-        r = at("fis", 0, 512, 1, 32 * k, 32 * k + 4)
-        dma("y", T.osc[4 * k:4 * k + 4, 0:512], ap(r), [at("fis", 0, 512)], [])
+        mm("P%d" % (4 + b), 128, EB, 128 * b, PP, 0)
+    left(2)
+    ts(at("nfin", 0, 32), at("nfin", 0, 32), col(X2), A.add, col(BO), A.subtract)
+    left(3)
+    tt(at("fo32", 0, 32), at("P1", C_FIN, C_FIN + 32), at("nfin", 0, 32), A.min)
+    ts(col(TH4, 4), col(K16, 4), col(M16), A.is_equal, 16.0, A.mult)
+    ts(at("fol", 0, 32), at("fo32", 0, 32), col(BO), A.add)
+    quant("qb", "qs", 0, OH, "lft", 0)
+    pick("fin", "fis", 0, "qb", "qs", 0, Q0 + 512, "fol", 0, 32)
     for b in range(4):
-        tt(at("lpt", b, 512, 4), at("at", b, 512, 4), at(pbank[b], 0, 128), A.subtract)
-    tt(at("go4", 0, 4), at("P7", 0, 4), at("cf", MK, MK + 4), A.add)
-    quant("pp", "pps", 128, 256, "lpt", 0)
+        tt(at("zt", b, 256, 4), at("fa", 256 + b, 512, 4), at("P%d" % (4 + b), 0, 64), A.subtract)
+    ts(at("zt", Z_X, Z_X + 16, 4, 0, 64), col(TH4, 4, 0, 64), at("rk2", 0, 1, 1, 0, 64), A.is_gt, float(NEW), A.mult)
+    cp(at("own", 0, 2), col(MK + 1, 2))
+    quant("pp", "pps", NEW, NEW + 128, "zt", 0)
+    mm("P7", 128, CT, C_W, PP, NEW)
+    quant("wq", "ws", 0, 128, "wt", 0)
+    mm("P0", 128, ("wq", "ws"), 0, ("w2", "w2s"), 16)
+    pick("l2", "l2s", 0, "w2", "w2s", 96, 144, "own", 0, 2)
+    act(at("yo", 16 * me, 16 * me + 16), at("P0", 112, 128), ACT.Copy)
+    tt(at("go4", 0, 4), at("P7", 64, 68), col(MK, 4), A.add)
     cp(at("gol", 0, 4), at("go4", 0, 4))
-    cp(col(OC), at("oci", 0, 1))
-    pick("gin", "gis", 0, "pp", "pps", 0, 256, "gol", 0, 4)
-    dma("y", T.oc[:, 2048:2304], codes(at("gin", 0, 64)), [at("gin", 0, 64)], [])
+    pick("fin", "fis", 512, "pp", "pps", 0, NEW + 128, "gol", 0, 4)
+    dma("y", T.oc[:], codes(at("fin", 0, 576)), [at("fin", 0, 576)], [])
     for k in range(4):
-        r = at("gis", 0, 64, 1, 32 * k, 32 * k + 4)
-        dma("y", T.osc[4 * k:4 * k + 4, 512:576], ap(r), [at("gis", 0, 64)], [])
+        r = at("fis", 0, 576, 1, 32 * k, 32 * k + 4)
+        dma("sy"[k % 2], T.osc[4 * k:4 * k + 4, :], ap(r), [at("fis", 0, 576)], [])
 
-    lands("arr2", n2, [at("l2", 0, 136), at("l2s", 0, 136)])
-    mm("P4", 128, ("wq", "ws"), 0, L2, 0)
-    mm("P5", 128, ("wq", "ws"), 0, L2, 8)
-    mm("P6", 128, L2, 0, CT, 112)
-    for o in range(4):
-        cp(at("yo", 16 * o, 16 * o + 16), at("P4", WIN * o + 1, WIN * o + 17))
-        act(at("yo", 64 + 16 * o, 80 + 16 * o), at("P5", WIN * (o + 4) - 7, WIN * (o + 4) + 9), ACT.Copy)
+    lands("arr2", 2 * (len(fe) * len(far) + len(ne)), [at("l2", L0 + WIN, L0 + N * WIN), at("l2s", L0 + WIN, L0 + N * WIN)])
+    a = L0 + N * WIN + 1 - 128
+    mm("P0", 128, ("wq", "ws"), 0, L2, a)
+    mm("P1", 128, ("wq", "ws"), 0, L2, a)
+    mm("P2", 128, L2, L0 - 1, CT, 0)
+    for j in range(1, N):
+        o, c = (me + j) % N, L0 + WIN * j + 1 - a
+        if j <= 5:
+            cp(at("yo", 16 * o, 16 * o + 16), at("P0", c, c + 16))
+        else:
+            act(at("yo", 16 * o, 16 * o + 16), at("P1", c, c + 16), ACT.Copy)
+    act(at("nbs", 0, 16), at("P2", C_NB, C_NB + 16), ACT.Copy)
     dma("y", T.y[:], ap(at("yo", 0, 128)), [at("yo", 0, 128)], [])
-    ts(at("nbs", 0, 16), at("P6", 0, 16), float(N), A.mult, col(OC), A.add)
-    dma("s", T.nb[0:1, 0:128], T.nbs[0:120:17, 0:16], [at("nbs", 0, 16)], [])
+    k = 1 + WIN * (N - me)
+    dma("s", T.nb[0:1, 16 * me:128], T.nbs[1:k - WIN + 1:WIN, 0:16], [at("nbs", 0, 16)], [])
+    if me:
+        dma("s", T.nb[0:1, 0:16 * me], T.nbs[k:121:WIN, 0:16], [at("nbs", 0, 16)], [])
     finish([("lcl", nloc[0])])

import numpy as np
from concourse.bass import DstId, RemoteDMATransfer
from concourse.mybir import dt, AluOpType, AxisListType, ActivationFunctionType

CODE = "float8_e4m3fn_x4"
BFT = "bfloat16"
F32 = "float32"
OH = 192
Q0 = OH + 264
V0 = 544
MSG = 18
OWN = 144
ZERO = 192
WIN = 17
L0 = 15
HD = 192
FS = 64
NEW = FS + 512
TINY = 2.0 ** -120
C_DOL, C_WIN, C_FIN, C_NB, C_W, C_END = 12, 76, 80, 112, 128, 264
Z_X, Z_OH, Z_NUM = 256, 272, 800

SCRATCH = {
    "ert": ("sbuf", [128, 2048], BFT), "grt": ("sbuf", [128, 2048], BFT), "fa": ("sbuf", [128, 512], BFT),
    "uc": ("sbuf", [128, 4], BFT), "ut": ("sbuf", [128, 512], BFT), "wt": ("sbuf", [128, 512], BFT),
    "ones": ("sbuf", [128, 128], BFT), "idn": ("sbuf", [128, 128], BFT), "eb": ("sbuf", [128, 516], BFT),
    "ebq": ("sbuf", [128, 512], CODE), "ebs": ("sbuf", [128, 512], "uint8"),
    "ci": ("sbuf", [128, 16], "int32"), "cf": ("sbuf", [128, 96], F32),
    "c64": ("sbuf", [128, 32], F32), "prm": ("sbuf", [128, 32], F32), "nfin": ("sbuf", [128, 32], F32),
    "one32": ("sbuf", [128, 128], F32), "lf": ("sbuf", [128, 128], F32), "lf2": ("sbuf", [128, 64], F32),
    "c4": ("sbuf", [128, 128], BFT), "m12": ("sbuf", [128, 12], F32),
    "i16": ("sbuf", [128, 144], BFT), "i16d": ("sbuf", [128, 256], BFT), "sm": ("sbuf", [128, 512 - HD], BFT),
    "ct": ("sbuf", [128, 4 * C_END], BFT), "ctq": ("sbuf", [128, C_END], CODE), "cts": ("sbuf", [128, C_END], "uint8"),
    "gl": ("sbuf", [128, 8], "uint16"), "lvo": ("sbuf", [128, 8], "uint16"),
    "erq": ("sbuf", [128, 512], CODE), "ers": ("sbuf", [128, 512], "uint8"),
    "uq": ("sbuf", [128, 128], CODE), "us": ("sbuf", [128, 128], "uint8"),
    "wq": ("sbuf", [128, 128], CODE), "ws": ("sbuf", [128, 128], "uint8"),
    "v": ("sbuf", [128, V0 + 2048], BFT), "qb": ("sbuf", [128, Q0 + 512], CODE), "qs": ("sbuf", [128, Q0 + 512], "uint8"),
    "zs": ("sbuf", [128, 512], F32), "a2": ("sbuf", [128, 128], F32), "a2t": ("sbuf", [128, 128], F32),
    "thr": ("sbuf", [128, 256], F32), "cmp": ("sbuf", [128, 256], F32), "junk": ("sbuf", [128, 128], F32),
    "rk": ("sbuf", [128, 4], F32), "oh1": ("sbuf", [128, 528], BFT),
    "ol": ("sbuf", [128, 12], "uint16"), "ol4": ("sbuf", [128, 48], "uint16"),
    "snd": ("sbuf", [128, 192], CODE), "sns": ("sbuf", [128, 192], "uint8"),
    "vs": ("sbuf", [128, 768], BFT), "lft": ("sbuf", [128, 768], BFT), "val": ("sbuf", [128, 8], F32),
    "fmw": ("sbuf", [128, 512], BFT), "fwq": ("sbuf", [128, 128], CODE), "fws": ("sbuf", [128, 128], "uint8"),
    "fo32": ("sbuf", [128, 32], F32), "fol": ("sbuf", [128, 32], "uint16"),
    "fin": ("sbuf", [128, 576], CODE), "fis": ("sbuf", [128, 576], "uint8"),
    "fs": ("sbuf", [128, 2048], BFT),
    "l1": ("sbuf", [128, ZERO + 128], CODE), "l1s": ("sbuf", [128, ZERO + 128], "uint8"),
    "lvq": ("sbuf", [128, 128], CODE), "lvs": ("sbuf", [128, 128], "uint8"),
    "dol": ("sbuf", [128, 32], "uint16"), "dq": ("sbuf", [128, 512], CODE), "dqs": ("sbuf", [128, 512], "uint8"),
    "so": ("sbuf", [128, 2048], BFT), "zt": ("sbuf", [128, 804], BFT),
    "xq": ("sbuf", [128, 132], CODE), "xs": ("sbuf", [128, 132], "uint8"),
    "pb": ("sbuf", [128, 128], CODE), "pbs": ("sbuf", [128, 128], "uint8"),
    "po4": ("sbuf", [128, 4], F32), "pol": ("sbuf", [128, 4], "uint16"),
    "pp": ("sbuf", [128, NEW + 128], CODE), "pps": ("sbuf", [128, NEW + 128], "uint8"),
    "sce2": ("sbuf", [128, 65], F32), "tt2": ("sbuf", [128, 64], F32),
    "cmp2": ("sbuf", [128, 64], F32), "rk2": ("sbuf", [128, 2], F32),
    "ohq": ("sbuf", [128, 128], CODE), "ohs": ("sbuf", [128, 128], "uint8"),
    "wol": ("sbuf", [128, 2], "uint16"), "own": ("sbuf", [128, 2], "uint16"),
    "w2": ("sbuf", [128, 144], CODE), "w2s": ("sbuf", [128, 144], "uint8"),
    "l2": ("sbuf", [128, 154], CODE), "l2s": ("sbuf", [128, 154], "uint8"),
    "go4": ("sbuf", [128, 4], F32), "gol": ("sbuf", [128, 4], "uint16"),
    "nbs": ("sbuf", [128, 16], F32), "yo": ("sbuf", [128, 128], F32),
}
for _k in range(8):
    SCRATCH["P%d" % _k] = ("psum", [128, 512], F32)
NDMA = 40
SEMAPHORES = ["v", "s", "t", "gp", "arr1", "arr2", "lcl"] + ["d%d" % i for i in range(NDMA)]


def at(name, a, b, st=1, p0=0, p1=128):
    return (name, a, b, st, p0, p1)


def hit(x, y):
    if x[0] != y[0] or x[4] >= y[5] or y[4] >= x[5] or x[1] >= y[2] or y[1] >= x[2]:
        return False
    return not (x[3] == y[3] and (x[1] - y[1]) % x[3] != 0)


def make_flow(g, T):
    queues = {"v": g.vector, "s": g.scalar, "t": g.tensor, "gp": g, "y": g.sync}
    count, know, hist, ndma = {}, {q: {} for q in queues}, {}, [0]

    def ap(r):
        return T[r[0]][r[4]:r[5], r[1]:r[2]] if r[3] == 1 else T[r[0]][r[4]:r[5], r[1]:r[2]:r[3]]

    def need(q, reads, writes, chain=False):
        toks = []
        for mode, rs in (("r", reads), ("w", writes)):
            for r in rs:
                for (q2, m2, r2, tok, ch) in hist.get(r[0], []):
                    bank = r[0][0] == "P"
                    if bank:
                        if q2 == q and m2 == "r" and mode == "r":
                            continue
                        if q2 == q and chain:
                            continue
                    elif (mode == "r" and m2 == "r") or not hit(r, r2):
                        continue
                    toks.append(tok)
        for sem, n, kn in sorted(toks, key=lambda x: -x[1]):
            if know[q].get(sem, 0) < n:
                queues[q].wait_ge(T.sem[sem], n)
                know[q][sem] = n
                for s2, n2 in kn.items():
                    know[q][s2] = max(know[q].get(s2, 0), n2)

    def note(q, reads, writes, tok, chain=False):
        for mode, rs in (("r", reads), ("w", writes)):
            for r in rs:
                h = hist.setdefault(r[0], [])
                if mode == "w" and not chain:
                    h[:] = [e for e in h if not (r[0][0] == "P" or (e[2][3] == 1 and r[3] == 1 and r[1] <= e[2][1]
                            and e[2][2] <= r[2] and r[4] <= e[2][4] and e[2][5] <= r[5]))]
                h.append((q, mode, r, tok, chain))

    def op(q, call, reads, writes, chain=False):
        need(q, reads, writes, chain)
        if q == "gp" and know[q].get(q, 0) < count.get(q, 0):
            g.wait_ge(T.sem[q], count[q])
            know[q][q] = count[q]
        ins = call()
        count[q] = count.get(q, 0) + 1
        ins.then_inc(T.sem[q], 1)
        note(q, reads, writes, (q, count[q], dict(know[q])), chain)

    def dma(q, out, in_, reads, writes):
        need(q, reads, writes)
        sem = "d%d" % ndma[0]
        ndma[0] += 1
        queues[q].dma_start(out, in_).then_inc(T.sem[sem], 16)
        count[sem] = 16
        note(q, reads, writes, (sem, 16, dict(know[q])))

    def lands(sem, n, writes):
        count[sem] = n
        note("far", [], writes, (sem, n, {}), True)

    def finish(extra):
        for sem, n in list(count.items()) + extra:
            if know["y"].get(sem, 0) < n:
                g.sync.wait_ge(T.sem[sem], n)

    return ap, need, op, dma, lands, finish


def ways(T, topo, src):
    far = [d for d in T.cores if topo.chip(d) != topo.chip(src)]
    near = [d for d in T.cores if topo.chip(d) == topo.chip(src) and d != src]
    e = topo.engines(src, far[0])
    return far, near, e, [x for x in topo.engines(src, near[0]) if x not in e][:2]


def plan1(T, topo, src, half, kind):
    far, near, e, ne = ways(T, topo, src)
    ds = [d for d in far if T.rank_of(d) % 2 == half]
    k = T.rank_of(src) // 2 % len(ds)
    ds = ds[k:] + ds[:k]
    n = len(e) // 4
    e = e[2 * n * kind:] + e[:2 * n * kind]
    return list(zip(ds, (e[:2 * n], e[2 * n:3 * n], e[3 * n:])))


def slot(o, first):
    return 96 * ((o + first) % 2) + 48 * (o // 4) + (30 if o // 2 % 2 else 0)


def bits(es):
    return sum(1 << x for x in es)


def rank_program(g, core, T, topo):
    me = T.rank_of(core)
    if me is None:
        return
    N = len(T.cores)
    ap, need, op, dma, lands, finish = make_flow(g, T)
    A = AluOpType
    ACT = ActivationFunctionType
    odd, quad = me % 2, me // 2
    q0, q1 = 32 * quad, 32 * quad + 32

    def ts(out, in0, s1, op0, s2=None, op1=None):
        reads = [in0] + [x for x in (s1, s2) if x is not None and not isinstance(x, (int, float))]
        a1 = s1 if isinstance(s1, (int, float)) else ap(s1)
        a2 = s2 if s2 is None or isinstance(s2, (int, float)) else ap(s2)
        if op1 is None:
            op("v", lambda: g.vector.tensor_scalar(ap(out), ap(in0), a1, None, op0), reads, [out])
        else:
            op("v", lambda: g.vector.tensor_scalar(ap(out), ap(in0), a1, a2, op0, op1), reads, [out])

    def tt(out, in0, in1, o):
        op("v", lambda: g.vector.tensor_tensor(ap(out), ap(in0), ap(in1), o), [in0, in1], [out])

    def cp(out, in_):
        op("v", lambda: g.vector.tensor_copy(ap(out), ap(in_)), [in_], [out])

    def fill(out, c):
        op("v", lambda: g.vector.memset(ap(out), c), [], [out])

    def total(out, in_):
        op("v", lambda: g.vector.tensor_reduce(ap(out), ap(in_), AxisListType.X, A.add), [in_], [out])

    def act(out, in_, f, bias=0.0, scale=1.0, acc=None):
        reads = [in_] + [x for x in (bias, scale) if not isinstance(x, float)]
        kw = {}
        if not (isinstance(bias, float) and bias == 0.0):
            kw["bias"] = bias if isinstance(bias, float) else ap(bias)
        if not (isinstance(scale, float) and scale == 1.0):
            kw["scale"] = scale if isinstance(scale, float) else ap(scale)
        if acc is not None:
            kw["accum_out"] = ap(acc)
        op("s", lambda: g.scalar.activation(ap(out), ap(in_), f, **kw), reads, [out] + ([acc] if acc else []))

    def lin(out, in_, scale, bias):
        act(out, in_, ACT.Identity, bias=bias, scale=scale)

    def quant(q, s, a, b, src, c):
        n = b - a
        i = at(src, c, c + 4 * n)
        op("v", lambda: g.vector.quantize_mx(ap(at(q, a, b)), ap(at(s, a, b)), ap(i)), [i], [at(q, a, b), at(s, a, b)])

    def mm(bank, n, w, a, x, b, start=True, stop=True):
        o, l, r = at(bank, 0, n), (at(w[0], a, a + 128), at(w[1], a, a + 128)), (at(x[0], b, b + n), at(x[1], b, b + n))
        op("t", lambda: g.tensor.matmul_mx(ap(o), ap(l[0]), ap(l[1]), ap(r[0]), ap(r[1]), start, stop),
           list(l) + list(r), [o], chain=not start)

    def pick(q2, s2, a2, q, s, a, b, off, e, f):
        n = 16 * (f - e)
        lst, wq, wsc, oq, osc = at(off, e, f), at(q, a, b), at(s, a, b), at(q2, a2, a2 + n), at(s2, a2, a2 + n)
        op("v", lambda: g.vector.tensor_copy(ap(oq).bitcast(dt.uint32), ap(wq).bitcast(dt.uint32).indirect(ap(lst))),
           [wq, lst], [oq])
        op("s", lambda: g.scalar.activation(ap(osc), ap(wsc).indirect(ap(lst)), ACT.Copy), [wsc, lst], [osc])

    def gather(out, win, lst):
        op("s", lambda: g.scalar.activation(ap(out), ap(win).indirect(ap(lst)), ACT.Copy), [win, lst], [out])

    def zeros(name, a, b):
        for c in range(a, b, 512):
            d = min(b, c + 512)
            act(at(name, c, d), at("eb", 0, d - c), ACT.Copy, scale=0.0)

    def codes(r):
        return ap(r).bitcast(dt.uint8)

    def load(q, t, a, b, x):
        dma(q, ap(at(t, a, b)), x, [], [at(t, a, b)])

    def iota(out, pattern, base, ch):
        if SCRATCH[out[0]][2] in (F32, BFT):
            op("gp", lambda: g.iota(ap(out), pattern, base, ch, allow_small_or_imprecise_dtypes=True), [], [out])
        else:
            op("gp", lambda: g.iota(ap(out), pattern, base, ch), [], [out])

    def select(out, in_, pattern, o, fillv, base, ch):
        op("gp", lambda: g.affine_select(ap(out), ap(in_), pattern, o, fillv, base, ch), [in_], [out])

    def col(a, n=1, p0=0, p1=128):
        return at("cf", a, a + n, 1, p0, p1)

    def whole(*ints):
        for a, m, s in ints:
            ts(at("ci", a, a + 1), at("ci", 0, 1), m, A.bitwise_and, s, A.arith_shift_right)
    P_, K_, A_, I_, B1, H_, S7, MD, E_, O2, KH, M16 = range(12)
    GL, M3, HI, NB, DL, C0, CON, LVC, BO, X1, X2, BF = range(12, 24)
    IT4, GP8, K16, TG, LO4, K64, MK, TH4, BM = 24, 32, 40, 44, 48, 52, 60, 64, 68
    EB, U, Q, CT, PP, L2 = ("ebq", "ebs"), ("uq", "us"), ("qb", "qs"), ("ctq", "cts"), ("pp", "pps"), ("l2", "l2s")
    far, near, fe, ne = ways(T, topo, core)
    nloc = [0]
    low = 1.0 - 2.0 ** -24
    first = 1 - odd
    e0, e1 = slot(me, first) // 32 * 2, (slot(me, first) + MSG + 15) // 16
    own = OWN + slot(me, first) - 16 * e0

    load("y", "ert", 0, 1024, T.er[:, 0:1024])
    load("s", "uc", 0, 4, T.u[:, 0:4])
    load("y", "ert", 1024, 2048, T.er[:, 1024:2048])
    for a, b in ((0, 1024), (1024, 1536), (1536, 2048)):
        load("y", "grt", a, b, T.gr[:, a:b])
    load("y", "fa", 0, 256, T.fo[:])
    load("y", "wt", 0, 512, T.w[:])

    fill(at("ones", 0, 128), 1.0)
    fill(at("eb", 0, 516), 0.0)
    iota(at("ci", 0, 1), [[0, 1]], 0, 1)
    select(at("idn", 0, 128), at("ones", 0, 128), [[-1, 128]], A.is_equal, 0.0, 0, 1)
    fill(at("one32", 0, 128), 1.0)
    whole((K_, 15, 0), (A_, 127, 5), (I_, 31, 0), (B1, 1, 0), (H_, 127, 6))
    cp(at("eb", 3, 515, 4), at("idn", 0, 128))
    zeros("ct", 0, 4 * C_W)
    cp(at("cf", 0, 6), at("ci", 0, 6))
    for b in range(4):
        quant("ebq", "ebs", 128 * b, 128 * b + 128, "eb", 3 - b)
    for buf, land, f in (("ebq", "l2", codes), ("ebs", "l2s", ap)):
        src, dst = at(buf, 0, 2), at(land, L0 + N * WIN, L0 + N * WIN + 2)
        dma("y", f(dst), f(src), [src], [dst])
    iota(at("m12", 0, 12), [[0, 2], [1, 6]], 0, 0)
    iota(col(LO4, 2), [[4, 2]], 1, 0)
    iota(col(BM, 2), [[-388, 2]], -1, 0)
    iota(col(GP8, 8), [[256, 2], [4, 2], [128, 2]], 0, 0)
    iota(at("i16d", 0, 256), [[0, 8], [1, 16], [0, 2]], 0, 0)
    for a in range(4):
        select(at("lf", 0, 128, 1, 32 * a, 32 * a + 32), at("one32", 0, 128, 1, 32 * a, 32 * a + 32),
               [[1, 2], [-1, 2], [-2, 32]], A.is_gt, low, 0, 2)
    iota(at("fs", 1536, 2048), [[0, 512]], 0, 0)
    iota(at("c64", 0, 32), [[1, 32]], 0, 0)
    iota(at("prm", 0, 32), [[4, 2], [8, 4], [1, 4]], 0, 0)
    iota(at("c4", 0, 128), [[1, 32], [0, 4]], 0, 0)
    iota(at("i16", 0, 144), [[0, 9], [1, 16]], 0, 0)
    iota(col(K16, 4), [[16, 4]], 0, 0)
    ts(col(M3), col(A_), 2.0, A.mult, col(H_), A.subtract)
    ts(col(NB), col(B1), -8.0, A.mult, col(A_), A.add)
    ts(col(HI), col(I_), col(B1), A.add, 8.0, A.mult)
    ts(at("m12", 0, 12), at("m12", 0, 12), col(M3), A.is_equal)
    ts(col(LO4, 2), col(LO4, 2), col(NB), A.add)
    ts(col(GL), col(K_), 8.0, A.mult, col(A_), A.add)
    ts(col(BM, 2), col(BM, 2), col(B1), A.add)
    ts(at("gl", 0, 8), col(GP8, 8), col(GL), A.add)
    zeros("v", 512, V0)
    zeros("oh1", 512, 528)
    for t in range(4):
        lin(at("ut", t, 512, 4), at("ones", 0, 128), 0.0, at("uc", t, t + 1))
    for b in range(2):
        act(at("ct", b, 48, 4), at("m12", 0, 12), ACT.Copy, scale=col(LO4 + b))
        act(at("ct", 2 + b, 48, 4), at("m12", 0, 12), ACT.Copy, scale=col(HI))
    for t in range(2):
        lin(at("ct", 4 + t, 48, 12, 0, 32), at("ones", 0, 4, 1, 0, 32), 0.0, -448.0)
    zeros("fs", 0, 1536)

    def unpack(i):
        quant("erq", "ers", 256 * i, 256 * i + 256, "ert", 1024 * i)
        for k in range(4):
            mm("P%d" % (4 * i + k), 256, EB, 128 * k, ("erq", "ers"), 256 * i)

    def vadd(a, b, h, *ks):
        c, i, h = V0 + 1024 * h, a // 256, (h + first) % 2
        for k in ks or range(4):
            tt(at("v", c + 2 * a + k, c + 2 * b, 4), at("P%d" % (4 * i + k), h + a - 256 * i, b - 256 * i, 2),
               at("grt", 4 * (a + h) + k, 4 * b, 8), A.add)

    def packed(a, b):
        quant("qb", "qs", Q0 + a, Q0 + b, "v", V0 + 4 * a)

    def scored(a, b, bk):
        mm(bk, b - a, U, 0, Q, Q0 + a)
        act(at("zs", a, b), at(bk, 0, b - a), ACT.Abs, bias=TINY)

    unpack(0)
    quant("uq", "us", 0, 128, "ut", 0)
    unpack(1)
    quant("ctq", "cts", 0, C_W, "ct", 0)
    vadd(0, 256, 0)
    vadd(0, 256, 1, 0)
    packed(0, 128)
    for k in range(4):
        vadd(256, 384, 0, k)
        vadd(384, 512, 0, k)
        if k < 3:
            vadd(0, 256, 1, k + 1)
    scored(0, 128, "P0")
    packed(128, 256)
    scored(128, 256, "P1")
    packed(256, 384)
    vadd(256, 512, 1)

    OHT = ("v", "oh1")
    LB = ("P6", "P7")

    def turned(h):
        o, i = at("a2t", 64 * h, 64 * h + 64), at("a2", 64 * h, 64 * h + 64)
        op("v", lambda: g.vector.transpose(ap(o), ap(i)), [i], [o])

    def limit(c):
        b, h = c // 2, c % 2
        tt(at("thr", 64 * c, 64 * c + 64), at("a2", 64 * h, 64 * h + 64), at("lf", 64 * b, 64 * b + 64), A.mult)

    def beats(c):
        a = 64 * (c % 2) + 32 * (c // 2)
        ts(at("cmp", 64 * c, 64 * c + 64), at("thr", 64 * c, 64 * c + 64), at("a2t", a, a + 1), A.is_ge)

    def count(c):
        if c % 2:
            act(at("junk", 32 * c - 32, 32 * c + 32), at("cmp", 64 * c, 64 * c + 64), ACT.Copy, acc=at("rk", c, c + 1))
        else:
            total(at("rk", c, c + 1), at("cmp", 64 * c, 64 * c + 64))

    def onehot(c):
        ts(at(OHT[c % 2], c // 2, 512, 2), at("i16d", 0, 256), at("rk", c, c + 1), A.is_equal)

    def rankcols(h):
        cp(at(OHT[h], 520, 528, 4), at("rk", h, 4, 2))
        act(at(OHT[h], 521, 528, 4), at("rk", h, 4, 2), ACT.Relu, bias=-15.0)

    def listed(h):
        a = OH + 132 * (1 - h)
        quant("qb", "qs", a, a + 132, OHT[h], 0)
        mm(LB[h], 128, Q, a, CT, 0)

    def offsets(h):
        ts(at("ol", 6 * h, 6 * h + 6), at(LB[h], 6 * h, 6 * h + 6), col(BM + h), A.max, float(Q0 - OH - 1 + 256 * h), A.add)

    def picked(h):
        pick("snd", "sns", 96 * h, "qb", "qs", OH, Q0 + 256 * (1 + h), "ol", 6 * h, 6 * h + 6)

    def sent(h):
        for kind, (buf, land, f) in enumerate((("snd", "l1", codes), ("sns", "l1s", ap))):
            trs, rs = [], []
            for d, es in plan1(T, topo, core, (h + first) % 2, kind) + [(near[0], ne)] * (h != kind):
                o = T.rank_of(d)
                r, l = at(buf, slot(o, first), slot(o, first) + MSG), at(land, MSG * me, MSG * me + MSG)
                rid, pid, _ = topo.addr(d)
                trs.append(RemoteDMATransfer(dst_ids=[DstId(rid=rid, pnc=pid)], dma_engine_mask=bits(es),
                                             remote_sem=T.sem.arr1, src=f(r), dst=f(l)))
                rs.append(r)
                nloc[0] += len(es)
            need("gp", rs, [])
            g.remote_dma_fused(trs, local_sem=T.sem.lcl)

    gather(at("a2", 0, 64), at("zs", 0, 256), at("gl", 0, 4))
    scored(256, 384, "P2")
    packed(384, 512)
    scored(384, 512, "P3")
    gather(at("a2", 64, 128), at("zs", 0, 512), at("gl", 4, 8))
    limit(0)
    turned(0)
    limit(2)
    beats(0)
    beats(2)
    count(0)
    count(2)
    onehot(0)
    onehot(2)
    rankcols(0)
    turned(1)
    listed(0)
    limit(1)
    limit(3)
    offsets(0)
    beats(1)
    picked(0)
    sent(0)
    count(1)
    beats(3)
    count(3)
    whole((S7, 7, 0), (MD, 56, 0))
    onehot(1)
    onehot(3)
    rankcols(1)
    for b in range(4):
        act(at("fs", b, 2048, 32), at("fa", b, 256, 4), ACT.Copy)
    listed(1)
    whole((E_, 15, 3), (O2, 7, 2), (KH, 15, 1))
    offsets(1)
    whole((M16, 48, 0))
    picked(1)
    sent(1)
    iota(col(IT4, 4), [[8, 2], [1 - 2 * first, 2]], first, 0)
    iota(col(K64, 4), [[16, 4]], 64, 0)
    iota(at("nfin", 0, 32), [[8, 32]], Q0, 0)
    select(at("lf2", 0, 64, 1, 0, 64), at("one32", 0, 64, 1, 0, 64), [[-1, 64]], A.is_gt, low, 0, 1)
    n1 = sum(len(es) for s in T.cores if s != core for kind in range(2)
             for d, es in plan1(T, topo, s, odd, kind) if d == core) + 2 * len(ne)

    def part(h):
        return (HD, 512) if h else (0, HD)

    def start(b, h):
        a, c = part(h)
        mm("P%d" % (4 * h + b), c - a, EB, 128 * b, PP, FS + a, True, False)
    for t in range(4):
        ts(at("ol4", 12 * t, 12 * t + 12), at("ol", 0, 12), 4.0, A.mult, float(V0 - 4 * (Q0 - OH) + t), A.add)
    for t in range(4):
        gather(at("vs", 192 * t, 192 * t + 192), at("v", 0, V0 + 2048), at("ol4", 12 * t, 12 * t + 12))
    quant("pp", "pps", FS, NEW, "fs", 0)
    for b in range(7):
        start(b % 4, b // 4)
    cp(at("cf", 6, 12), at("ci", 6, 12))
    fill(at("zt", Z_X, Z_NUM + 4), 0.0)
    ts(col(DL), col(S7), float(me), A.is_equal, float(own - MSG * me), A.mult)
    pick("l1", "l1s", OWN, "qb", "qs", OH, Q0 + 512, "ol", e0, e1)
    quant("l1", "l1s", ZERO, ZERO + 128, "zt", Z_OH)
    ts(col(C0), col(S7), float(MSG), A.mult, col(DL), A.add)
    lin(col(CON), col(C0), 1.0, 2.0 if quad % 2 else 0.0)
    lin(at("zt", Z_OH, Z_OH + 16, 4, 32, 64), col(K16, 4, 32, 64), 0.5, 0.0)
    lin(col(MK, 4), col(K16, 4), 1.0, col(K_))
    lin(col(BF), col(B1), 1.0 - 2 * first, float(first))
    lin(col(X1), col(B1), -1.0, col(S7))
    lin(col(X2), col(BF), 256.0, col(KH))
    ts(col(LVC), col(C0), col(E_), A.add, 0.0 if quad % 2 else 16.0, A.add)
    for t, c in ((0, 1.0), (1, 256.0)):
        for a, src in ((4 * C_DOL, "c64"), (4 * C_DOL + 128, "prm")):
            ts(at("ct", a + t, a + 128, 4, q0, q1), at(src, 0, 32, 1, q0, q1), col(I_, 1, q0, q1), A.is_equal, c, A.mult)
    ts(at("lvo", 0, 8), at("c64", 0, 8), 0.0, A.mult, col(LVC), A.add)
    ts(at("ct", 4 * C_FIN, 4 * C_FIN + 128), at("c4", 0, 128), col(I_), A.is_equal)
    ts(at("ct", 4 * C_NB, 4 * C_NB + 64), at("c4", 0, 64), col(P_), A.is_equal)
    cp(at("ct", 4 * C_WIN, 4 * C_WIN + 8, 4, 0, 64), col(S7, 2, 0, 64))
    fill(at("sm", 0, 512 - HD), 1.0)
    quant("ctq", "cts", 0, C_W, "ct", 0)
    fill(at("sm", 0, 512 - HD, 8), 0.0)
    fill(at("ct", 4 * C_W, 4 * C_END, 1, 0, 64), 0.0)
    for t in range(4):
        ts(at("ct", 4 * C_W + t, 4 * C_END, 4, 64, 128), at("i16", 0, 136, 1, 64, 128), 2.0 * t, A.subtract,
           col(E_, 1, 64, 128), A.is_equal)
    ts(at("ct", 4 * C_W, 4 * C_W + 512, 4, 0, 64), at("i16", 0, 128, 1, 0, 64), col(K_, 1, 0, 64), A.is_equal)
    fill(at("zt", Z_NUM + 2, Z_NUM + 3), float(me))
    quant("ctq", "cts", C_W, C_END, "ct", 4 * C_W)

    lands("arr1", n1, [at("l1", 0, OWN), at("l1s", 0, OWN)])
    pick("lvq", "lvs", 0, "l1", "l1s", 0, ZERO + 128, "lvo", 0, 8)
    mm("P7", 128, ("lvq", "lvs"), 0, CT, 0)
    ts(at("val", 4, 8), at("rk", 0, 4), 16.0, A.is_ge, 1024.0, A.mult)
    ts(col(TG, 4), col(IT4, 4), col(A_), A.add, col(A_), A.add)
    tt(at("val", 0, 4), at("val", 4, 8), at("rk", 0, 4), A.max)
    ts(col(X1), col(X1), col(O2), A.subtract, 16.0, A.mult)
    ts(at("dol", 0, 32), at("P7", C_DOL, C_DOL + 32), col(CON), A.add, float(ZERO), A.min)
    DQ = ("dq", "dqs")

    def dense(b, h):
        a, c = part(h)
        mm("P%d" % (4 * h + b), c - a, EB, 128 * b, DQ, a, False, True)

    def scan(b, h):
        a, c = part(h)
        o, d0, d1 = at("so", 512 * b + a, 512 * b + c), at("sm", 0, c - a), at("P%d" % (4 * h + b), 0, c - a)
        op("v", lambda: g.vector.tensor_tensor_scan(ap(o), ap(d0), ap(d1), 0.0, A.mult, A.add), [d0, d1], [o])
        if h and b < 3:
            act(at("fa", 256 + b, 512, 4), at("so", 512 * b + 7, 512 * b + 512, 8), ACT.Copy)
    ts(at("zt", Z_OH, Z_OH + 32, 1, 64, 128), at("P7", C_DOL + 32, C_DOL + 64, 1, 64, 128), 16.0, A.is_lt, 64.0, A.mult)
    start(3, 1)
    pick("dq", "dqs", 0, "l1", "l1s", 0, ZERO + 128, "dol", 0, HD // 16)
    for b in range(4):
        dense(b, 0)
    pick("dq", "dqs", HD, "l1", "l1s", 0, ZERO + 128, "dol", HD // 16, 32)
    for b in range(4):
        dense(b, 1)
    for b in range(4):
        scan(b, 0)
    quant("xq", "xs", 0, 132, "zt", Z_OH)
    mm("P0", 128, CT, C_W, ("xq", "xs"), 0, True, False)
    mm("P0", 128, CT, C_W + 8, ("xq", "xs"), 4, False, True)
    for b in range(4):
        scan(b, 1)
    tt(at("po4", 0, 4), at("P0", 0, 4), col(K64, 4), A.min)
    cp(at("fa", 259, 512, 4), at("so", 1543, 2048, 8))
    ts(at("pol", 0, 4), at("po4", 0, 4), col(K_), A.add)
    quant("pb", "pbs", 0, 128, "fa", 0)
    pick("pp", "pps", 0, "pb", "pbs", 0, 128, "pol", 0, 4)

    def rest(b):
        mm("P%d" % b, 192, EB, 128 * b, ("snd", "sns"), 0)

    def left(b):
        tt(at("lft", b, 768, 4), at("vs", 192 * b, 192 * b + 192), at("P%d" % b, 0, 192), A.subtract)

    def kept(t):
        ts(at("fmw", t, 512, 4), at("i16", 0, 128), col(TG + t), A.is_equal, at("val", t, t + 1), A.mult)
    rest(1)
    mm("P5", 128, U, 0, PP, 0)
    mm("P4", 128, PP, 0, U, 0)
    act(at("sce2", 0, 64, 1, 0, 64), at("P5", 0, 64, 1, 0, 64), ACT.Abs, bias=TINY)
    act(at("sce2", 64, 65, 1, 0, 64), at("P4", 0, 1, 1, 0, 64), ACT.Abs, bias=TINY)
    rest(0)
    rest(2)
    left(1)
    lin(col(BO), col(BF), 96.0, col(X1))
    for t in range(3):
        kept(t)
    tt(at("tt2", 0, 64, 1, 0, 64), at("sce2", 0, 64, 1, 0, 64), at("lf2", 0, 64, 1, 0, 64), A.mult)
    ts(at("cmp2", 0, 64, 1, 0, 64), at("tt2", 0, 64, 1, 0, 64), at("sce2", 64, 65, 1, 0, 64), A.is_ge)
    total(at("rk2", 0, 1, 1, 0, 64), at("cmp2", 0, 64, 1, 0, 64))
    ts(at("zt", Z_OH, Z_OH + 512, 4, 0, 64), at("i16", 0, 128, 1, 0, 64), at("rk2", 0, 1, 1, 0, 64), A.is_equal)
    quant("ohq", "ohs", 0, 128, "zt", Z_OH)
    mm("P6", 128, ("ohq", "ohs"), 0, CT, 0)
    rest(3)
    left(0)
    kept(3)
    ts(at("zt", Z_NUM, Z_NUM + 2), at("P6", C_WIN, C_WIN + 2), float(N), A.mult)
    ts(at("wol", 0, 1), at("P6", C_WIN, C_WIN + 1), at("P6", C_WIN + 1, C_WIN + 2), A.add)
    quant("w2", "w2s", 0, 128, "zt", Z_NUM + 4 - 512)
    pick("w2", "w2s", 128, "pp", "pps", 0, 128, "wol", 0, 1)

    def home(land, o, d):
        a = L0 + WIN * ((o - d) % N)
        return at(land, a, a + WIN)
    for buf, land, f in (("w2", "l2", codes), ("w2s", "l2s", ap)):
        src = at(buf, 127, 144)
        trs = []
        k = 2 * (quad % 3)
        for ds, es in ((far[k:] + far[:k], fe), (near, ne)):
            ids = [DstId(rid=topo.addr(d)[0], pnc=topo.addr(d)[1]) for d in ds]
            trs.append(RemoteDMATransfer(dst_ids=ids, dma_engine_mask=bits(es), remote_sem=T.sem.arr2, srcs=[f(src)],
                                         dsts=[f(home(land, me, T.rank_of(d))) for d in ds]))
        need("gp", [src], [])
        g.remote_dma_fused(trs, local_sem=T.sem.lcl)
        nloc[0] += len(fe) + len(ne)

    quant("fwq", "fws", 0, 128, "fmw", 0)
    mm("P1", 128, ("fwq", "fws"), 0, CT, 0)
    for b in range(4):
        mm("P%d" % (4 + b), 128, EB, 128 * b, PP, 0)
    left(2)
    ts(at("nfin", 0, 32), at("nfin", 0, 32), col(X2), A.add, col(BO), A.subtract)
    left(3)
    tt(at("fo32", 0, 32), at("P1", C_FIN, C_FIN + 32), at("nfin", 0, 32), A.min)
    ts(col(TH4, 4), col(K16, 4), col(M16), A.is_equal, 16.0, A.mult)
    ts(at("fol", 0, 32), at("fo32", 0, 32), col(BO), A.add)
    quant("qb", "qs", 0, OH, "lft", 0)
    pick("fin", "fis", 0, "qb", "qs", 0, Q0 + 512, "fol", 0, 32)
    for b in range(4):
        tt(at("zt", b, 256, 4), at("fa", 256 + b, 512, 4), at("P%d" % (4 + b), 0, 64), A.subtract)
    ts(at("zt", Z_X, Z_X + 16, 4, 0, 64), col(TH4, 4, 0, 64), at("rk2", 0, 1, 1, 0, 64), A.is_gt, float(NEW), A.mult)
    cp(at("own", 0, 2), col(MK + 1, 2))
    quant("pp", "pps", NEW, NEW + 128, "zt", 0)
    mm("P7", 128, CT, C_W, PP, NEW)
    quant("wq", "ws", 0, 128, "wt", 0)
    mm("P0", 128, ("wq", "ws"), 0, ("w2", "w2s"), 16)
    pick("l2", "l2s", 0, "w2", "w2s", 96, 144, "own", 0, 2)
    act(at("yo", 16 * me, 16 * me + 16), at("P0", 112, 128), ACT.Copy)
    tt(at("go4", 0, 4), at("P7", 64, 68), col(MK, 4), A.add)
    cp(at("gol", 0, 4), at("go4", 0, 4))
    pick("fin", "fis", 512, "pp", "pps", 0, NEW + 128, "gol", 0, 4)
    dma("y", T.oc[:], codes(at("fin", 0, 576)), [at("fin", 0, 576)], [])
    for k in range(4):
        r = at("fis", 0, 576, 1, 32 * k, 32 * k + 4)
        dma("sy"[k % 2], T.osc[4 * k:4 * k + 4, :], ap(r), [at("fis", 0, 576)], [])

    lands("arr2", 2 * (len(fe) * len(far) + len(ne)), [at("l2", L0 + WIN, L0 + N * WIN), at("l2s", L0 + WIN, L0 + N * WIN)])
    a = L0 + N * WIN + 1 - 128
    mm("P0", 128, ("wq", "ws"), 0, L2, a)
    mm("P1", 128, ("wq", "ws"), 0, L2, a)
    mm("P2", 128, L2, L0 - 1, CT, 0)
    for j in range(1, N):
        o, c = (me + j) % N, L0 + WIN * j + 1 - a
        if j <= 5:
            cp(at("yo", 16 * o, 16 * o + 16), at("P0", c, c + 16))
        else:
            act(at("yo", 16 * o, 16 * o + 16), at("P1", c, c + 16), ACT.Copy)
    act(at("nbs", 0, 16), at("P2", C_NB, C_NB + 16), ACT.Copy)
    dma("y", T.y[:], ap(at("yo", 0, 128)), [at("yo", 0, 128)], [])
    k = 1 + WIN * (N - me)
    dma("s", T.nb[0:1, 16 * me:128], T.nbs[1:k - WIN + 1:WIN, 0:16], [at("nbs", 0, 16)], [])
    if me:
        dma("s", T.nb[0:1, 0:16 * me], T.nbs[k:121:WIN, 0:16], [at("nbs", 0, 16)], [])
    finish([("lcl", nloc[0])])
